import numpy as np, ml_dtypes
CORES = [3,7,11,15,131,135,139,143]
N = 8
import mx_ref
BF = ml_dtypes.bfloat16
def gentries(a):
    return np.ascontiguousarray(a.reshape(8, 16, -1).transpose(0, 2, 1)).reshape(8, -1)
def gtable(e):
    e = np.asarray(e); return np.ascontiguousarray(e.reshape(8, -1, 16).transpose(0, 2, 1)).reshape(128, -1).astype(np.int32)
def cols(t, e):
    v = np.concatenate([t.reshape(128, -1, 4), np.zeros((128, 1, 4), BF)], axis=1)
    return np.ascontiguousarray(v[:, e]).reshape(128, -1)
def gcols(t, e):
    v = np.concatenate([t.reshape(8, 16, -1, 4), np.zeros((8, 16, 1, 4), BF)], axis=2)
    return np.ascontiguousarray(np.stack([v[g][:, e[g]] for g in range(8)])).reshape(128, -1)
def tile(rs):
    return np.stack(rs, axis=2).reshape(128, -1).astype(BF)
def cut(t, i, w=512):
    return t[:, w * i:w * i + w]
def pick(q, e):
    c = np.concatenate([q[0].reshape(128, -1, 4), np.zeros((128, 1, 4), np.uint8)], axis=1); s = np.concatenate([q[1], np.ones((16, 1), np.uint8)], axis=1)
    return (np.ascontiguousarray(c[:, e].reshape(128, -1)), np.ascontiguousarray(s[:, e]))
def join(*qs):
    return (np.concatenate([q[0] for q in qs], axis=1), np.concatenate([q[1] for q in qs], axis=1))
def put(q, e, v):
    c, s = q[0].reshape(128, -1, 4).copy(), q[1].copy(); c[:, e] = v[0].reshape(128, -1, 4); s[:, e] = v[1]
    return (c.reshape(128, -1), s)
def pk(c, s):
    return (np.ascontiguousarray(c), mx_ref.live(s))
def emit(q):
    return q[0], q[1]
def packed(v, rng):
    q = [mx_ref.quantize(np.ascontiguousarray(v[r])) for r in range(N)]
    return np.stack([a for a, b in q]), np.stack([mx_ref.plane(b, rng) for a, b in q])
def values_of_codes():
    e, c = np.zeros((128, 128, 4), np.float32), np.zeros((128, 2, 4), np.uint8)
    e[np.arange(128), np.arange(128), 0] = 1
    c[:127, :, 0] = np.arange(256).reshape(2, 128).T[:127]
    return mx_ref.matmul(mx_ref.quantize(e.reshape(128, 512).astype(BF)), (c.reshape(128, 8), np.full((16, 2), 127, np.uint8))).T.reshape(-1).astype(np.float64)
CODE_VALUE, SCALE_VALUE = values_of_codes(), 2.0 ** (np.arange(256) - 127.0)
def decode(q):
    return (CODE_VALUE[q[0]].reshape(16, 8, -1, 4) * SCALE_VALUE[q[1]][:, None, :, None] + 0.0).reshape(128, -1).astype(np.float32)
def f(rng, *shape):
    return mx_ref.flush((rng.standard_normal(shape, dtype=np.float32) * np.exp2(rng.integers(-2, 3, shape[:-1] + (1,)))).astype(BF))
def wide(rng, *shape, cols=0):
    v = rng.standard_normal(shape, dtype=np.float32) * np.exp2(rng.integers(-12, 13, shape)).astype(np.float32)
    if cols: v *= np.repeat(np.exp2(rng.integers(-cols, cols + 1, shape[:-2] + (1, shape[-1] // 4))) * (rng.random(shape[:-2] + (1, shape[-1] // 4)) > 0.0625), 4, axis=-1).astype(np.float32)
    return mx_ref.flush(v.astype(BF))
MC, P, A, K, R = 768, 256, 192, 32, 3
def numbers_of(rng):
    return {"m": np.array(f(rng, N, 128, 4 * MC)), "x": np.array(f(rng, N, 128, 4 * P)), "u": np.array(f(rng, N, 128, 512)), "v": np.array(f(rng, N, 128, 512))}
def weights(rng, w):
    c, p = packed(w, rng)
    return {"wc": c, "ws": p}
def still(rng):
    w = np.zeros((N, 128, 4, 128, 4), np.float32)
    i = np.arange(128)
    for b in range(4): w[:, i, b, i, b] = 32
    return weights(rng, w.reshape(N, 128, 2048).astype(BF))
def signs(rng):
    return np.stack([rng.permutation(8) % 2 * 2.0 - 1.0 for r in range(N)])
def mixed(rng, t):
    n = rng.integers(0, 2 * K + 1, (R, 8))
    n[0] = rng.permutation(np.concatenate([[0, K - 1, K, K + 1, 2 * K], n[0, :3]]))
    o = []
    for g in range(8):
        known = t[g]
        for i in range(R):
            new = np.setdiff1d(np.arange(MC), known)
            e = rng.permutation(np.concatenate([rng.choice(known, A - n[i, g], replace=False), rng.choice(new, n[i, g], replace=False)]))
            o.append(e)
            known = np.union1d(known, e)
    return np.stack(o).reshape(8, R * A)
def exact(rng, t, n):
    o, sure, out = [], t, np.setdiff1d(np.arange(MC), t)
    for i in range(R):
        e = rng.permutation(np.concatenate([rng.choice(sure, A - n, replace=False), rng.choice(out, n, replace=False)]))
        miss = np.isin(e, out)
        served = e[miss][:K]
        sure = np.concatenate([e[~miss], served])
        out = np.setdiff1d(out, served)
        o.append(e)
    return np.concatenate(o)
def draw_tags(rng):
    return np.stack([np.stack([rng.permutation(MC)[:P] for g in range(8)]) for r in range(N)])
def lists_of(rng):
    t = draw_tags(rng)
    return {"tg": np.stack([gtable(t[r]) for r in range(N)]), "ad": np.stack([gtable(mixed(rng, t[r])) for r in range(N)])}
def held(l, r):
    t, a = gentries(l["tg"][r]), gentries(l["ad"][r])[:, :A]
    return np.stack([np.isin(t[g], a[g]) for g in range(8)])
def fine(rng, v, s):
    v = v.astype(np.float32).reshape(N, 8, 16, -1, 4)
    g = ((s[..., None] >> np.arange(8)) & 1) * np.exp2(np.arange(8) - 23.0)
    v[:, :, 0] = 0
    v[:, :, 0, :, 0] = 1
    v[:, :, 8] = g[..., :4]
    v[:, :, 9] = g[..., 4:]
    a = v[:, :, 10:].shape
    v[:, :, 10:] = rng.integers(4, 8, a) * rng.choice([-1.0, 1.0], a) * 2.0 ** -20
    return v.reshape(N, 128, -1).astype(BF)
def setup_inputs(rng):
    return {**numbers_of(rng), **weights(rng, f(rng, N, 128, 2048)), **lists_of(rng)}
def setup_inputs_full(rng):
    d = {**numbers_of(rng), **weights(rng, f(rng, N, 128, 2048))}
    t = draw_tags(rng)
    e = rng.permutation(N)
    ad = []
    for r in range(N):
        kind = rng.permutation(8)
        o = []
        for g in range(8):
            if r == e[0]: o.append(exact(rng, t[r, g], A))
            elif r == e[1]: o.append(exact(rng, t[r, g], 0))
            elif kind[g] < 6: o.append(exact(rng, t[r, g], [0, 1, K - 1, K, K + 1, A][kind[g]]))
            elif kind[g] == 6: o.append(rng.permutation(MC)[:R * A])
            else: o.append(np.concatenate([rng.choice(np.setdiff1d(np.arange(MC), t[r, g]), A, replace=False)] + [rng.choice(t[r, g], A, replace=False) for i in range(R - 1)]))
        ad.append(gtable(np.stack(o)))
    return {**d, "tg": np.stack([gtable(t[r]) for r in range(N)]), "ad": np.stack(ad)}
def setup_inputs_ties(rng):
    d = setup_inputs(rng)
    e = rng.permutation(N)
    for r in range(N):
        k = np.zeros(P, int) if r == e[0] else rng.permutation(P) % 3
        d["x"][r] = cols(d["x"][r], np.where(k == 2, -1, k))
    o = (e[0] + 1) % N
    d["m"][o] = cols(d["m"][o], np.zeros(MC, int))
    d["x"][e[1]] = 0
    return d
def setup_inputs_near(rng):
    d = numbers_of(rng)
    l = lists_of(rng)
    g = signs(rng)
    down = (P - 1 - np.arange(P)) // 2
    s = np.tile(down, (N, 8, 1))
    r = int(rng.integers(N))
    hit = held(l, r)
    for i in range(8): s[r, i, np.argsort(hit[i], kind="stable")] = down
    u = d["u"].reshape(N, 128, 128, 4)
    u[:, :, ::16] = 0
    for h in range(0, 128, 16):
        u[:, h, h, 0] = g[:, h // 16].astype(BF)
        u[:, h + 8:h + 10, h] = 1
    return {"m": fine(rng, d["m"], rng.integers(0, P // 2, (N, 8, MC))), "x": fine(rng, d["x"], s), "u": u.reshape(N, 128, 512), "v": d["v"], **still(rng), **l}
def setup_inputs_huge(rng):
    d = numbers_of(rng)
    l = lists_of(rng)
    g = signs(rng)
    m = 2.0 ** 30 * (0.6 + 0.4 * rng.random((N, 128, 4 * MC), dtype=np.float32))
    x = 2.0 ** 30 * (0.6 + 0.4 * rng.random((N, 128, 4 * P), dtype=np.float32))
    a = 2.0 ** 30 * (1 - 0.25 * rng.random((N, 128, 8, 4)))
    c = np.stack([rng.permutation(P) % 2 * 2.0 - 1.0 for r in range(N)])
    e = rng.permutation(N)
    c[e[:N // 2]] = 1
    r = e[-1]
    hit = held(l, r)
    k = int(np.argmax(np.sum(hit, axis=1) == A - K))
    c[r] = np.where(hit[k], -g[r, k], g[r, k])
    x[r] = 2.0 ** 30
    a[r] = 2.0 ** 30
    x = x * np.repeat(c, 4, axis=1)[:, None, :]
    u = d["u"].reshape(N, 128, 128, 4)
    a = a * g[:, None, :, None]
    u[:, :, ::16] = a.astype(np.float32).astype(BF)
    return {"m": m.astype(np.float32).astype(BF), "x": x.astype(np.float32).astype(BF), "u": u.reshape(N, 128, 512), "v": d["v"], **still(rng), **l}
def setup_inputs_spread(rng):
    d = setup_inputs(rng)
    d["m"] = np.array(wide(rng, N, 128, 4 * MC, cols=6))
    d["x"] = np.array(wide(rng, N, 128, 4 * P, cols=6))
    r = int(rng.integers(N))
    t, a = gentries(d["tg"][r]), gentries(d["ad"][r])[:, :A]
    g = int(np.argmax([np.sum(~np.isin(a[i], t[i])) for i in range(8)]))
    size = np.full(P, 2.0 ** -24)
    size[rng.choice(np.flatnonzero(~np.isin(t[g], a[g])), 16, replace=False)] = 2.0 ** 20
    v = f(rng, 128, 4 * P).astype(np.float32) * np.repeat(size, 4).astype(np.float32)
    d["x"][r] = mx_ref.flush(v.astype(BF))
    return d
def check_inputs(d):
    b = []
    for k in ("m", "x", "u", "v"):
        a = np.abs(d[k].astype(np.float32))
        if not (np.isfinite(a).all() and ((a == 0) | (a >= 2.0 ** -30) & (a <= 2.0 ** 30)).all()): b.append("a value of " + k)
    t = np.stack([gentries(a) for a in d["tg"]])
    if (t < 0).any() or (t >= MC).any(): b.append("a tag out of range")
    if (np.diff(np.sort(t, axis=-1), axis=-1) == 0).any(): b.append("a tag twice in a cache")
    a = np.stack([gentries(a) for a in d["ad"]]).reshape(N, 8, R, A)
    if (a < 0).any() or (a >= MC).any(): b.append("an address out of range")
    if (np.diff(np.sort(a, axis=-1), axis=-1) == 0).any(): b.append("an address twice in a round of a cache")
    return b
def reference(m, x, u, v, wc, ws, tg, ad):
    qu = [mx_ref.quantize(u[r]) for r in range(N)]
    lay = [pk(wc[r], ws[r]) for r in range(N)]
    now = [x[r] for r in range(N)]
    tags = [np.array(gentries(tg[r])) for r in range(N)]
    acc = [gentries(ad[r]).reshape(8, R, A) for r in range(N)]
    for t in range(R):
        source, target, fetched = [], [], []
        for r in range(N):
            marks = mx_ref.matmul(qu[r], mx_ref.quantize(now[r]))[::16] + np.float32(0.0)
            ask = np.full((8, K), -1)
            src = np.full((8, A), -1)
            dst = np.full((8, A), -1)
            for g in range(8):
                want = acc[r][g, t]
                at = np.full(MC, -1)
                at[tags[r][g]] = np.arange(P)
                place = at[want]
                miss = np.flatnonzero(place < 0)[:K]
                n = len(miss)
                order = np.argsort(marks[g], kind="stable")
                victims = order[~np.isin(order, place)][:n]
                ask[g, :n] = want[miss]
                src[g] = place
                src[g, miss] = P + np.arange(n)
                dst[g] = place
                dst[g, miss] = victims
                tags[r][g, victims] = want[miss]
            source.append(src)
            target.append(dst)
            fetched.append(mx_ref.quantize(gcols(m[(r + 1) % N], ask)))
        came = decode(join(*fetched)).astype(BF)
        for r in range(N):
            z = mx_ref.quantize(gcols(np.concatenate([now[r], cut(came, r, 4 * K)], axis=1), source[r]))
            h = tile([np.maximum(mx_ref.matmul(pick(lay[r], np.arange(128 * b, 128 * b + 128)), z), np.float32(0.0)) * np.float32(0.03125) for b in range(4)])
            e = np.tile(np.arange(P), (8, 1))
            g, j = np.nonzero(target[r] >= 0)
            e[g, target[r][g, j]] = P + j
            now[r] = gcols(np.concatenate([now[r], h], axis=1), e)
    y, ot = np.zeros((N, 128, P), np.float32), np.zeros((N, 8, P), np.float32)
    oc, osc = np.zeros((N, 128, 4 * P), np.uint8), np.zeros((N, 16, P), np.uint8)
    for r in range(N):
        q = mx_ref.quantize(now[r])
        y[r] = mx_ref.matmul(mx_ref.quantize(v[r]), q)
        ot[r] = tags[r]
        oc[r], osc[r] = emit(q)
    return {"y": y, "ot": ot, "oc": oc, "osc": osc}

@@ -1,0 +1,412 @@
+from concourse.bass import DstId, RemoteDMATransfer
+from concourse.mybir import dt, AluOpType as OP, ActivationFunctionType as AF
+
+MC, P, A, K, R = 768, 256, 192, 32, 3
+CODE, U8, U16, BF, F32, I32 = "float8_e4m3fn_x4", "uint8", "uint16", "bfloat16", "float32", "int32"
+XB = [36, 36, 204]
+DB = [3, 3, 11]
+XW = P + A + K
+HZ = XW - P
+SPLIT = [8, 8, 8]
+ORDER = """
+0y 1s 2y 3s 4y 5y 6y 7g 10v 9g 15v 12s 11v 21s 13v 14v 26v 25v 16v 57v 32s 20s 53v 66s 17g 52v 55v 35g 54v 34s 56v 58g 64v 65s 106v 28s 78v 79s 24v
+80v 67v 84v 27s 33s 107p 108v 19s 83s 18g 85v 86s 110v 87s 109v 144s 135s 8g 22v 153s 88v 23v 145s 150s 89v 180v 90v 136s 46g 138s 151s 141s 81v 152s
+91v 82v 36g 29s 143s 92v 96g 30s 168v 147s 174v 159v 166v 119v 139s 155s 140s 156s 137s 169v 154s 163v 165v 148s 162v 158s 38g 185s 59x 160v 171v 63s
+172v 61s 69v 173v 51v 161v 50v 182v 120v 170v 181v 175v 45g 60s 37g 167v 62s 39g 72s 184s 188v 178v 97x 177v 183v 142s 98s 146s 99v 164v 190v 100g
+101x 179v 157s 186v 149s 75s 176v 191v 193v 192v 187v 40g 94s 194v 195v 197s 121v 49v 115p 31s 198v 199v 210s 208v 209v 47v 211v 309s 68s 43g 212v
+122v 111p 213v 214v 216s 48v 244v 215s 218v 217v 219v 220v 189v 221v 102g 224g 196v 117p 116s 112s 118s 71v 104y 113p 114s 310s 42g 123s 124s 125v
+127p 312v 204v 74s 245v 126p 311v 246v 129p 133v 206v 131s 200v 313v 130s 128p 132s 134s 207s 247v 202v 225x 226v 227v 205s 203s 73s 76s 201v 231v
+314v 70s 95s 232p 233v 235v 234v 293v 281s 288v 294v 287v 228g 272s 278s 263s 260s 307v 296v 229g 230x 240p 269s 280s 264s 242p 308v 261s 300v 284v
+77v 265s 285v 290v 291v 299v 305v 315v 297v 266s 301v 306v 279s 303v 302v 286v 271s 274s 273s 298v 283s 241v 243v 267s 238p 239v 236p 268s 237v 103x
+105v 248v 262s 353p 275s 249s 292v 270s 250v 295v 251p 252p 289v 282s 304v 223v 277s 253p 276s 316v 359p 254p 318v 317v 319v 255s 222v 320v 357p 322v
+256s 321v 323v 331v 324v 329v 333v 257s 325v 258s 259s 330s 334v 327v 332s 326s 336v 328s 44g 337v 348v 41g 354s 338v 335s 355p 339v 356s 349p 350v
+341s 430v 428s 351v 352v 361s 362v 429s 340s 343v 397s 93s 342v 391s 382s 363v 403v 432v 400s 385s 364v 421v 394s 383s 416v 409v 404v 344v 398s 424v
+396s 393s 388s 401s 365v 406v 418v 379s 380s 426v 366v 422v 415v 360s 358s 419v 367v 402s 431v 345v 407v 427v 413v 405v 399s 417v 389s 368s 386s 369v
+410v 373p 346v 434v 420v 371p 392s 408v 412v 411v 425v 423v 384s 381s 414v 395s 387s 390s 435v 437v 436v 433v 370p 438v 439v 372p 440v 446v 450v 444v
+375s 448v 377s 376s 374s 378s 447v 451s 449s 445v 452v 459g 347s 453p 460s 462s 441v 457y 442v 455y 443v 454v 458g 456y 461s
+"""
+PLAN = [(int(w[:-1]), w[-1]) for w in ORDER.split()]
+PER_ROUND = {"jm": (P, F32), "jd": (P, F32), "oj": (16, U16), "hm": (P, F32), "m2": (P, F32), "pv": (P, F32), "kk": (P, F32),
+             "nm": (A, BF), "c2": (A, BF), "sj": (2 * A, BF), "js": (2, F32), "jo": (4, U16), "gm": (64, F32), "gs": (64, F32), "ls": (16, U16),
+             "s3": (A, BF), "s4": (A, BF), "s5": (A, BF), "zo": (48, U16), "eqd": (P, BF), "cor": (P, BF), "ra": (16, F32), "gb": (16, F32),
+             "d": (16 * 12, F32), "th": (2, F32), "tpf": (16, F32), "tpu": (16, U16), "xo": (64, U16), "inv": (MC, F32), "zz": (4 * A, BF)}
+
+
+def _sb(n, d):
+    return ("sbuf", [128, n], d)
+
+
+SCRATCH = {
+    "tg32": _sb(16, I32), "ad32": _sb(36, I32), "tgu": _sb(16, U16), "adu": _sb(36, U16),
+    "l2s": _sb(48, U16), "l2r": _sb(48, U16), "lr0": _sb(8, U16), "lr1": _sb(8, U16),
+    "mt": _sb(4 * MC, BF), "ft": _sb(4 * 256, BF), "fq": _sb(224, CODE), "fs": _sb(224, U8), "f1q": _sb(128, CODE), "f1s": _sb(128, U8),
+    "lq": _sb(384, CODE), "lsn": _sb(384, U8), "zt": _sb(512, BF),
+    "strip": _sb(528, BF), "eq": _sb(512, CODE), "es": _sb(512, U8),
+    "ut": _sb(512, BF), "vt": _sb(512, BF), "uq0": _sb(128, CODE), "us0": _sb(128, U8), "uq": _sb(128, CODE), "us": _sb(128, U8),
+    "vq": _sb(128, CODE), "vs": _sb(128, U8), "uoff": _sb(8, U16), "wq": _sb(512, CODE), "wsn": _sb(512, U8),
+    "xt0": _sb(4 * (XB[0] + XW), BF), "xt1": _sb(4 * (XB[1] + XW), BF), "xt2": _sb(4 * (XB[2] + XW), BF), "xt3": _sb(4 * P, BF),
+    "xq": _sb(P, CODE), "xs": _sb(P, U8), "zq": _sb(A, CODE), "zs": _sb(A, U8),
+    "iot": _sb(MC, F32), "ones": _sb(MC, BF), "at0": _sb(MC, BF), "acc0": _sb(208, BF), "acc1": _sb(976, BF), "acc2": _sb(976, BF),
+    "n33": _sb(A, BF), "prow": _sb(P, BF), "jrow": _sb(A, BF), "s1": _sb(A, BF), "s2": _sb(A, BF),
+    "pat16": _sb(P, BF), "pat4": _sb(A, BF), "mask16": _sb(P, BF), "keep16": _sb(P, BF), "c16": _sb(P, BF), "r16": _sb(P, BF),
+    "mask4": _sb(A, BF), "keep4": _sb(A, BF),
+    "pi": _sb(4, I32), "pj": _sb(4, I32), "pc": _sb(8, F32), "kc": _sb(2, F32), "pd": _sb(16, F32), "pdm": _sb(16, F32), "cb": _sb(48, F32),
+    "jw1": _sb(288, F32), "jw2": _sb(320, F32), "ir01": _sb(A, F32), "ir02": _sb(A, F32), "ir12": _sb(A, F32),
+    "tw": _sb(352, F32), "aw": _sb(4 * A, F32), "cmp": _sb(16 * P, BF), "cnt": _sb(16 * 128, BF),
+    "yb": _sb(P, F32), "otb": _sb(P, F32),
+    "ps": ("psum", [128, 4096], F32),
+}
+for _n in PER_ROUND:
+    SCRATCH[_n] = _sb(R * PER_ROUND[_n][0], PER_ROUND[_n][1])
+LOADS = ["tg", "ad", "x", "u", "m", "wc", "ws", "v"]
+SEMAPHORES = ["cv", "cs", "cp", "cg", "sent", "a_l2", "a_l0", "a_l1", "a_f0", "a_f2", "a_f1", "st1", "st2", "st3"] + ["ld_" + n for n in LOADS]
+
+
+def calls(g, core, T, topo):
+    rank, n = T.rank_of(core), len(T.cores)
+    owner, asker = T.cores[(rank + 1) % n], T.cores[(rank - 1) % n]
+    nodes, wrote, read = [], {}, {}
+
+    def node(rd, wr, alts, sem=None, inc=1, arrival=None):
+        rd, wr = rd.split(), wr.split()
+        deps = set(wrote[k] for k in rd if k in wrote)
+        for k in wr:
+            deps |= set(read.get(k, []))
+            if k in wrote:
+                deps.add(wrote[k])
+        i = len(nodes)
+        nodes.append({"deps": sorted(deps), "alts": alts, "sem": sem, "inc": inc, "arrival": arrival})
+        for k in rd:
+            read.setdefault(k, []).append(i)
+        for k in wr:
+            wrote[k] = i
+            read[k] = []
+        return i
+
+    def lanes(src, dst):
+        return topo.engines(src, dst)[:8]
+
+    def bits(es):
+        return sum(1 << e for e in es)
+
+    def send(dst, src, sem, rd, lands, size, pairs, before=0):
+        rid, pid = topo.addr(dst, core)
+        es = lanes(core, dst)
+
+        def f(e):
+            if len(pairs) == 1:
+                return e.remote_dma(pairs[0][0], pairs[0][1], T.sem[sem], T.sem.sent, pid, rid, bits(es))
+            h = len(es) // 2
+            return e.remote_dma_fused([RemoteDMATransfer(dst_ids=[DstId(rid=rid, pnc=pid)], dma_engine_mask=bits(es[h * i:h * i + h]), remote_sem=T.sem[sem],
+                                                         src=pairs[i][1], dst=pairs[i][0]) for i in range(2)], local_sem=T.sem.sent)
+        node(rd + " wire", "wire sent_" + sem, {"g": (f, "send", size)}, sem="sent", inc=len(es))
+        if lands:
+            node("sent_" + sem, lands, {"x": (None, "far", size)}, arrival=(sem, (1 + before) * len(lanes(src, core))))
+
+    def V(rd, wr, f, kind, size):
+        node(rd, wr, {"v": (f, kind, size)})
+
+    def ts(rd, wr, out, a, s1, o1, s2=None, o2=None, c=64):
+        if s2 is None:
+            V(rd, wr, lambda e: e.tensor_scalar(out, a, s1, None, o1), "e", c)
+        else:
+            V(rd, wr, lambda e: e.tensor_scalar(out, a, s1, s2, o1, o2), "e", c)
+
+    def tt(rd, wr, out, a, b, o, c=64, kind="e"):
+        V(rd, wr, lambda e: e.tensor_tensor(out, a, b, o), kind, c)
+
+    def cp(rd, wr, out, a, c=64, kind="e"):
+        V(rd, wr, lambda e: e.tensor_copy(out, a), kind, c)
+
+    def scan(rd, wr, out, a, b, init, o0, o1, c):
+        V(rd, wr, lambda e: e.tensor_tensor_scan(out, a, b, init, o0, o1), "e", c)
+
+    def quant(rd, wr, q, s, a, cols):
+        V(rd, wr, lambda e: e.quantize_mx(q, s, a), "q", 4 * cols)
+
+    def act(rd, wr, out, a, f, c=64, kind="e", **kw):
+        node(rd, wr, {"s": (lambda e: e.activation(out, a, f, **kw), kind, c)})
+
+    def move(rd, wr, out, a, c, kind="ga"):
+        node(rd, wr, {"s": (lambda e: e.activation(out, a, AF.Copy), kind, c), "v": (lambda e: e.tensor_copy(out, a), kind, c)})
+
+    def lin(rd, wr, out, a, scale, bias, c=64):
+        node(rd, wr, {"s": (lambda e: e.activation(out, a, AF.Identity, scale=scale, bias=bias), "e", c),
+                      "v": (lambda e: e.tensor_scalar(out, a, scale, bias, OP.mult, OP.add), "e", c)})
+
+    def steps(wr, out, width, base, step=0, only=None):
+        alts = {"g": (lambda e: e.iota(out, [[step, width]], base, 0, allow_small_or_imprecise_dtypes=True), "g", width)}
+        if step == 0:
+            alts["v"] = (lambda e: e.memset(out, float(base)), "e", width // 2)
+        if only:
+            alts = {only: alts[only]}
+        node("", wr, alts)
+
+    def mm(rd, bank, w, ws, x, xs, cols):
+        node(rd, "ps%d" % bank, {"p": (lambda e: e.matmul_mx(T.ps[:, 512 * bank:512 * bank + cols], w, ws, x, xs, True, True), "mm", cols)})
+
+    def dma(q, sem, rd, wr, out, a, size):
+        node(rd, wr, {q: (lambda e: e.dma_start(out, a), "dma", size)}, sem=sem, inc=16)
+
+    def B(name, t, a=0, b=None, step=1):
+        w = PER_ROUND[name][0]
+        return T[name][:, w * t + a:w * t + (w if b is None else b):step]
+
+    xt = [T.xt0, T.xt1, T.xt2, T.xt3]
+    acc = [T.acc0[:, 0:A], T.acc1[:, 1:A + 1], T.acc2[:, 1:A + 1]]
+    jw = [None, T.jw1, T.jw2]
+    adu = [T.adu[:, 12 * t:12 * t + 12] for t in range(R)]
+    xbase = [4 * XB[0], 4 * XB[1], 4 * XB[2], 0]
+    MARKS = 0
+    pm = T.ps[:, 512 * MARKS:512 * MARKS + P]
+
+    dma("y", "ld_tg", "q1", "q1 tg32", T.tg32[:], T.tg[:], 8192)
+    dma("s", "ld_ad", "", "ad32", T.ad32[:], T.ad[:], 18432)
+    dma("y", "ld_x", "", "X0", T.xt0[:, xbase[0]:xbase[0] + 4 * P], T.x[:], 280000)
+    dma("s", "ld_u", "", "ut", T.ut[:], T.u[:], 420000)
+    dma("y", "ld_m", "", "mt", T.mt[:], T.m[:], 1200000)
+    dma("y", "ld_wc", "", "wq", T.wq[:].bitcast(dt.uint8), T.wc[:], 1460000)
+    dma("y", "ld_ws", "", "wsn", T.wsn[:], T.ws[:], 1530000)
+
+    node("", "pi", {"g": (lambda e: e.iota(T.pi[:, 0:1], [[0, 1]], 0, 1), "g", 1)})
+    node("", "pat4", {"g": (lambda e: e.iota(T.pat4[:], [[0, A // 4], [1, 4]], 0, 0, allow_small_or_imprecise_dtypes=True), "g", A)})
+    node("", "pat16", {"g": (lambda e: e.iota(T.pat16[:], [[0, 16], [1, 16]], 0, 0, allow_small_or_imprecise_dtypes=True), "g", P)})
+    steps("ones", T.ones[:], MC, 1, only="v")
+    scan("ones", "iot", T.iot[:], T.ones[:], T.ones[:], -1.0, OP.add, OP.mult, MC)
+    lin("ones", "at0", T.at0[:], T.ones[:], 0.0, -64.0, MC)
+    ts("pi", "pj0", T.pj[:, 0:1], T.pi[:, 0:1], 15, OP.bitwise_and)
+    ts("pi", "pj1", T.pj[:, 1:2], T.pi[:, 0:1], 3, OP.bitwise_and)
+    ts("pi", "pj2", T.pj[:, 2:3], T.pi[:, 0:1], 2, OP.logical_shift_right, 3, OP.bitwise_and)
+    cp("pj0 pj1 pj2", "pc", T.pc[:, 0:3], T.pj[:, 0:3])
+    steps("prow", T.prow[:], P, 1, 1)
+    steps("n33", T.n33[:], A, -33)
+    lin("pc", "kc0", T.kc[:, 0:1], T.pc[:, 0:1], -1.0, 31.5)
+    lin("pc", "kc1", T.kc[:, 1:2], T.pc[:, 0:1], -1.0, 15.5)
+    move("iot", "awi", T.aw[:, 0:A], T.iot[:, 0:A], A, "e")
+    ts("pc pat4", "mask4", T.mask4[:], T.pat4[:], T.pc[:, 2:3], OP.is_equal, c=96)
+    ts("pat4", "keep4", T.keep4[:], T.pat4[:], 0.0, OP.not_equal, c=96)
+    ts("pc pat16", "mask16", T.mask16[:], T.pat16[:], T.pc[:, 0:1], OP.is_equal, c=128)
+    ts("pat16", "keep16", T.keep16[:], T.pat16[:], 0.0, OP.not_equal, c=128)
+    cp("iot", "uoff", T.uoff[:], T.iot[:, 0:128:16])
+    lin("mask16", "c16", T.c16[:], T.mask16[:], -9e29, 4.5e29, P)
+    lin("keep16", "r16", T.r16[:], T.keep16[:], -9e29, 4.5e29, P)
+    lin("iot pc", "pd", T.pd[:], T.iot[:, 0:P:16], 1.0, T.pc[:, 0:1])
+    lin("pd", "pdm", T.pdm[:], T.pd[:], 1.0, -255.0)
+    lin("pc", "zc0", T.pc[:, 4:5], T.pc[:, 1:2], 1.0, 4.0 * (XB[0] - 1))
+    lin("pc", "zc2", T.pc[:, 5:6], T.pc[:, 1:2], 1.0, 4.0 * (XB[2] - 1))
+    for a in sorted(set(SPLIT)):
+        o = 16 * SPLIT.index(a)
+        lin("iot", "cbs%d" % a, T.cb[:, o:o + a], T.iot[:, 0:a], -16.0, float(HZ - 16))
+        lin("iot", "cbv%d" % a, T.cb[:, o + a:o + 16], T.iot[:, a:16], 0.0, float(HZ))
+    for t in range(R):
+        steps("inv%d" % t, B("inv", t), MC, A + 1, 1)
+    steps("zt", T.zt[:], 512, 0)
+    steps("D0", T.xt0[:, 0:xbase[0]], xbase[0], 0)
+    steps("D1", T.xt1[:, 0:xbase[1]], xbase[1], 0)
+    steps("D2", T.xt2[:, 0:4 * DB[2]], 4 * DB[2], 0)
+    steps("D2z", T.xt2[:, xbase[2] - 4:xbase[2]], 4, 0)
+    steps("acc1", acc[1], A, -64)
+    steps("acc2", acc[2], A, -512)
+    steps("jrow", T.jrow[:], A, -A, 1)
+    node("ones", "strip", {"g": (lambda e: e.affine_select(T.strip[:], T.ones[:, 0:528], [[1, 528]], OP.is_equal, 0.0, -3, -4), "g", 550)})
+    for b in range(4):
+        quant("strip", "eq%d" % b, T.eq[:, 128 * b:128 * b + 128], T.es[:, 128 * b:128 * b + 128], T.strip[:, 3 - b:3 - b + 512], 128)
+    quant("zt", "lZ", T.lq[:, 32:160], T.lsn[:, 32:160], T.zt[:], 128)
+
+    cp("tg32", "tgu", T.tgu[:], T.tg32[:])
+    cp("ad32", "adu", T.adu[:], T.ad32[:])
+    for e in range(4):
+        ts("ad32", "l2s%d" % e, T.l2s[:, 12 * e:12 * e + 12], T.ad32[:, 24:36], 4.0, OP.mult, float(e), OP.add)
+    send(owner, asker, "a_l2", "l2s0 l2s1 l2s2 l2s3", "l2r", 12288, [(T.l2r[:], T.l2s[:])])
+    for e in range(4):
+        move("mt l2r", "F2%d" % e, T.ft[:, 256 + e:1024:4], T.mt[:].indirect(T.l2r[:, 12 * e:12 * e + 12]), A)
+    cp("tgu prow", "at0", T.at0[:].indirect(T.tgu[:]), T.prow[:], P, "sc")
+    move("at0 adu", "acc0", acc[0], T.at0[:].indirect(adu[0]), A)
+    for t in range(R):
+        move("iot adu", "aw%d" % t, T.aw[:, A * (t + 1):A * (t + 2)], T.iot[:].indirect(adu[t]), A)
+        cp("iot adu", "inv%d" % t, B("inv", t).indirect(adu[t]), T.iot[:, 1:A + 1], A, "sc")
+    move("inv1 adu", "ir01", T.ir01[:], B("inv", 1).indirect(adu[0]), A)
+    move("inv2 adu", "ir02", T.ir02[:], B("inv", 2).indirect(adu[0]), A)
+    move("inv2 adu", "ir12", T.ir12[:], B("inv", 2).indirect(adu[1]), A)
+    move("inv1 tgu", "jw1a", T.jw1[:, 0:P], B("inv", 1).indirect(T.tgu[:]), P)
+    move("inv2 tgu", "jw2a", T.jw2[:, 0:P], B("inv", 2).indirect(T.tgu[:]), P)
+    move("iot tgu", "twa", T.tw[:, 0:P], T.iot[:].indirect(T.tgu[:]), P)
+    quant("ut", "uq0", T.uq0[:], T.us0[:], T.ut[:], 128)
+    move("uq0 uoff", "us", T.us[:], T.us0[:].indirect(T.uoff[:]), 128)
+    cp("uq0 uoff", "uq", T.uq[:].bitcast(dt.uint32), T.uq0[:].bitcast(dt.uint32).indirect(T.uoff[:]), 128, "ga")
+
+    def unpack(t):
+        a, cols = [(64, 128), (0, 128), (192, 192)][t]
+        o, w = [(96, K), (0, K), (0, A)][t]
+        rd = ["lZ lF0", "lZ lF1", "lF0 lF2"][t]
+        for b in range(4):
+            mm(rd + " eq%d" % b, 4 + b, T.eq[:, 128 * b:128 * b + 128], T.es[:, 128 * b:128 * b + 128], T.lq[:, a:a + cols], T.lsn[:, a:a + cols], cols)
+            e, c = 4 * DB[t], 512 * (4 + b) + o
+            move("D%d" % t, "ps%d D%d%d" % (4 + b, t, b), xt[t][:, e + b:e + 4 * w:4], T.ps[:, c:c + w], w, "e")
+
+    def marks(t):
+        quant("X%d X%d0 X%d1 X%d2 X%d3" % ((t,) * 5), "xq", T.xq[:], T.xs[:], xt[t][:, xbase[t]:xbase[t] + 4 * P], P)
+        if t < 3:
+            mm("xq uq us", MARKS, T.uq[:], T.us[:], T.xq[:], T.xs[:], P)
+        else:
+            mm("xq vq", MARKS, T.vq[:], T.vs[:], T.xq[:], T.xs[:], P)
+
+    def one_round(t):
+        def k(s):
+            return s.replace("#", str(t))
+
+        def D(i, a=0, b=16):
+            return B("d", t, 16 * i + a, 16 * i + b)
+
+        JD, a = B("jd", t, 15, P, 16), SPLIT[t]
+        if t == 0:
+            rd, src = "inv0 tgu", B("inv", 0).indirect(T.tgu[:])
+        else:
+            rd, src = k("jw#a jw#b jw#c tpu%d" % (t - 1)), jw[t][:].indirect(B("tpu", t - 1))
+        tt(rd + " mask16", k("jm#"), B("jm", t), src, T.mask16[:], OP.mult, P, "ga")
+        scan(k("jm# keep16"), k("jd#"), B("jd", t), T.keep16[:], B("jm", t), 0.0, OP.mult, OP.add, P)
+        act(rd, k("hm#"), B("hm", t), src, AF.Relu, P, "ga", scale=-1e27, bias=192.5e27)
+        if t > 0:
+            cp(k("jd#"), k("oj#"), B("oj", t), JD)
+            cp(k("oj# prow"), k("acc#"), T["acc%d" % t][:].indirect(B("oj", t)), T.prow[:], P, "sc")
+        ts(k("acc#"), k("nm#"), B("nm", t), acc[t], 0.0, OP.is_lt, -1.0, OP.mult, 96)
+        scan(k("nm# n33"), k("c2#"), B("c2", t), B("nm", t), T.n33[:], 0.0, OP.add, OP.max, 96)
+        for i in range(2):
+            act(k("c2# kc%d" % i), k("js#%d" % i), B("sj", t, A * i, A * i + A - 1), B("c2", t, 0, A - 1), AF.Sign, A + 20, bias=T.kc[:, i:i + 1],
+                accum_out=B("js", t, i, i + 1))
+        ts(k("js#0 js#1"), k("joa#"), B("jo", t, 0, 2), B("js", t), 0.5, OP.mult, 95.5 + A * (t + 1), OP.add)
+        ts(k("js#0 js#1"), k("job#"), B("jo", t, 2, 4), B("js", t), 0.5, OP.mult, 95.5, OP.add)
+        rd = "awi " + " ".join("aw%d" % i for i in range(t + 1))
+        tt(rd + k(" joa# job# mask4"), k("gm#"), B("gm", t), T.aw[:, 0:A * (t + 2)].indirect(B("jo", t)), T.mask4[:, 0:64], OP.mult, 64, "ga")
+        scan(k("gm# keep4"), k("gs#"), B("gs", t), T.keep4[:, 0:64], B("gm", t), 0.0, OP.mult, OP.add, 64)
+        ts(k("gs# pc"), k("ls#"), B("ls", t), B("gs", t, 3, 64, 4), 4.0, OP.mult, T.pc[:, 1:2], OP.add)
+        jk = B("jo", t, 2, 4)
+        move(k("aw# job#"), k("tw#"), T.tw[:, P + K * t:P + K * t + K], T.aw[:, A * (t + 1):A * (t + 2)].indirect(jk), K)
+        if t == 0:
+            move("ir01 job0", "jw1b", T.jw1[:, P:P + K], T.ir01[:].indirect(jk), K)
+            move("ir02 job0", "jw2b", T.jw2[:, P:P + K], T.ir02[:].indirect(jk), K)
+            send(owner, asker, "a_l0", "ls0", "lr0", 2048, [(T.lr0[:], B("ls", 0, 0, 8))])
+            move("mt lr0", "F0", T.ft[:, 128:256], T.mt[:].indirect(T.lr0[:]), 128)
+            quant("F0 F20 F21 F22 F23", "fq", T.fq[:], T.fs[:], T.ft[:, 128:1024], 224)
+            send(asker, owner, "a_f0", "fq", "lF0", 57344, [(T.lq[:, 160:216].bitcast(dt.uint8), T.fq[:, 0:56].bitcast(dt.uint8)), (T.lsn[:, 160:384], T.fs[:])])
+            send(asker, owner, "a_f2", "fq", "lF2", 143000, [(T.lq[:, 216:384].bitcast(dt.uint8), T.fq[:, 56:224].bitcast(dt.uint8))])
+            dma("y", "ld_v", "lF0", "vt", T.vt[:], T.v[:], 131072)
+            quant("vt", "vq", T.vq[:], T.vs[:], T.vt[:], 128)
+        if t == 1:
+            move("ir12 job1", "jw2c", T.jw2[:, P + K:P + 2 * K], T.ir12[:].indirect(jk), K)
+            send(owner, asker, "a_l1", "ls1", "lr1", 2048, [(T.lr1[:], B("ls", 1, 0, 8))])
+            move("mt lr1", "F1", T.ft[:, 0:128], T.mt[:].indirect(T.lr1[:]), 128)
+            quant("F1 F0 F20 F21 F22 F23", "f1q", T.f1q[:], T.f1s[:], T.ft[:, 0:512], 128)
+            send(asker, owner, "a_f1", "f1q", "", 16384, [(T.lq[:, 0:K].bitcast(dt.uint8), T.f1q[:, 0:K].bitcast(dt.uint8))])
+            send(asker, owner, "a_f1", "f1q", "lF1", 20480, [(T.lsn[:, 0:K], T.f1s[:, 0:K])], before=1)
+        marks(t)
+        tt("c16", k("m2# ps%d" % MARKS), B("m2", t), pm, T.c16[:], OP.max, P)
+        tt(k("hm#"), k("kk# ps%d" % MARKS), B("kk", t), pm, B("hm", t), OP.add, P)
+        scan(k("m2# r16"), k("pv#"), B("pv", t), T.r16[:], B("m2", t), 0.0, OP.max, OP.min, P)
+        unpack(t)
+        if t < 2:
+            tt(k("acc# c2#"), k("s3#"), B("s3", t), acc[t], B("c2", t), OP.max, 2 * A)
+        else:
+            lin("c22", "s1", T.s1[:], B("c2", t), 400.0, 13000.0, A)
+            tt("s1 jrow", "s2", T.s2[:], T.s1[:], T.jrow[:], OP.min, 2 * A)
+            tt("acc2 s2", "s32", B("s3", t), acc[t], T.s2[:], OP.max, 2 * A)
+        tt(k("s3# mask4"), k("s4#"), B("s4", t), B("s3", t), T.mask4[:], OP.mult, 2 * A)
+        scan(k("s4# keep4"), k("s5#"), B("s5", t), T.keep4[:], B("s4", t), 0.0, OP.mult, OP.add, 96)
+        c = 4 if t < 2 else 5
+        ts(k("s5# zc0 zc2"), k("zo#"), B("zo", t), B("s5", t, 3, A, 4), 4.0, OP.mult, T.pc[:, c:c + 1], OP.add)
+        for h in range(2):
+            move(k("zo# D# D#z D#0 D#1 D#2 D#3 X# X#0 X#1 X#2 X#3"), k("zz#%d" % h), B("zz", t, 384 * h, 384 * h + 384),
+                 xt[t][:, 0:xbase[t] + 4 * P].indirect(B("zo", t, 24 * h, 24 * h + 24)), 384)
+        quant(k("zz#0 zz#1"), "zq", T.zq[:], T.zs[:], B("zz", t), A)
+        e = xbase[t] + 4 * P
+        for b in range(4):
+            mm("zq wq wsn", b, T.wq[:, 128 * b:128 * b + 128], T.wsn[:, 128 * b:128 * b + 128], T.zq[:], T.zs[:], A)
+        for b in range(4):
+            out, src = xt[t][:, e + b:e + 4 * A:4], T.ps[:, 512 * b:512 * b + A]
+            node("", k("ps%d H#%d" % (b, b)), {"s": (lambda q, out=out, src=src: q.activation(out, src, AF.Relu, scale=0.03125), "e", A),
+                                               "v": (lambda q, out=out, src=src: q.tensor_scalar(out, src, 0.0, 0.03125, OP.max, OP.mult), "e", A)})
+        move(k("H#0 H#1 H#2 H#3 ls#"), k("HS#"), xt[t][:, e + 4 * A:e + 4 * A + 4 * K], xt[t][:, e:e + 4 * A].indirect(B("ls", t, 8, 16)), 128)
+        for c in range(16):
+            h, piv, o = 16 * c + 16, B("pv", t, 16 * c + 15, 16 * c + 16), P * c
+            lo, hi = T.cmp[:, o:o + h], T.cmp[:, o + h:o + P]
+            if c < a:
+                act(k("kk# pv#"), "cma%d cmb%d" % (c, c), T.cmp[:, o:o + P], B("kk", t), AF.Sign, P, scale=-1.0, bias=piv)
+                act("", k("cma%d gb#_%d" % (c, c)), lo, lo, AF.Relu, max(64, h) + 20, scale=-1.0, accum_out=B("gb", t, c, c + 1))
+                act("", k("cmb%d ra#_%d" % (c, c)), hi, hi, AF.Relu, max(64, P - h) + 20, accum_out=B("ra", t, c, c + 1))
+            else:
+                ts(k("kk# pv#"), "cma%d" % c, lo, B("kk", t, 0, h), piv, OP.is_le, c=h)
+                if h < P:
+                    ts(k("kk# pv#"), "cmb%d" % c, hi, B("kk", t, h, P), piv, OP.is_lt, c=P - h)
+                scan("cma%d cmb%d" % (c, c), "cnt%d" % c, T.cnt[:, 128 * c:128 * c + 128], T.cmp[:, o:o + 128], T.cmp[:, o + 128:o + P], 0.0, OP.add, OP.add, 64)
+        tt(k("pv# kk#"), k("eqd#"), B("eqd", t), B("pv", t), B("kk", t), OP.is_equal, 2 * P)
+        scan(k("eqd# keep16"), k("cor#"), B("cor", t), T.keep16[:], B("eqd", t), 0.0, OP.mult, OP.add, 128)
+        act(k("jd#"), k("d0#"), D(0), JD, AF.Relu, scale=4000.0, bias=-192.5 * 4000.0)
+        act(k("jd#"), k("d1#"), D(1), JD, AF.Relu, scale=-2000.0, bias=192.5 * 2000.0)
+        ts(k("c2#"), k("th#"), B("th", t, 0, 1), B("c2", t, A - 1, A), -32.0, OP.max, HZ + 0.5, OP.add)
+        tt(k("jd# d0#"), k("d2#"), D(2), JD, D(0), OP.subtract)
+        o = 16 * SPLIT.index(a)
+        tt(k("d1# cbs%d cbv%d" % (a, a)), k("d3#"), D(3), T.cb[:, o:o + 16], D(1), OP.subtract)
+        tt(k("d2# pdm"), k("d4#"), D(4), D(2), T.pdm[:], OP.max)
+        tt(k("d3# cor#"), k("d5#"), D(5), D(3), B("cor", t, 15, P, 16), OP.add)
+        tt(k(" ".join("gb#_%d ra#_%d" % (c, c) for c in range(a))), k("d6#"), D(6, 0, a), B("gb", t, 0, a), B("ra", t, 0, a), OP.subtract)
+        tt(k("d5# d6#"), k("d7a#"), D(7, 0, a), D(5, 0, a), D(6, 0, a), OP.add)
+        tt(k("d5# ") + " ".join("cnt%d" % c for c in range(a, 16)), k("d7b#"), D(7, a), D(5, a), T.cnt[:, 128 * a + 127:2048:128], OP.subtract)
+        ts(k("d7a# d7b# th#"), k("d8#"), D(8), D(7), B("th", t, 0, 1), OP.subtract, 4096.0, OP.mult)
+        tt(k("d7a# d7b# d8#"), k("d9#"), D(9), D(7), D(8), OP.min)
+        tt(k("d9# d4#"), k("d10#"), D(10), D(9), D(4), OP.max)
+        lin(k("d9#"), k("d11#"), D(11), D(9), 1.0, float(P + K - 1 - HZ + K * t))
+        tt(k("d11# pd tpf%d" % (t - 1)), k("tpf#"), B("tpf", t), D(11), T.pd[:] if t == 0 else B("tpf", t - 1), OP.max)
+        cp(k("tpf#"), k("tpu#"), B("tpu", t), B("tpf", t))
+        for e in range(4):
+            ts(k("d10#"), k("xo#%d" % e), B("xo", t, 16 * e, 16 * e + 16), D(10), 4.0, OP.mult, 4.0 * (P - 1) + e, OP.add)
+            move(k("X# X#0 X#1 X#2 X#3 H#0 H#1 H#2 H#3 HS# xo#%d" % e), "X%d%d" % (t + 1, e), xt[t + 1][:, xbase[t + 1] + e:xbase[t + 1] + 4 * P:4],
+                 xt[t][:, xbase[t]:xbase[t] + 4 * XW].indirect(B("xo", t, 16 * e, 16 * e + 16)), P)
+
+    for t in range(R):
+        one_round(t)
+
+    marks(3)
+    move("twa tw0 tw1 tw2 tpu2", "otb", T.otb[:], T.tw[:].indirect(B("tpu", 2)), P)
+    dma("y", "st1", "xq", "", T.oc[:], T.xq[:].bitcast(dt.uint8), 131072)
+    for i in range(4):
+        dma("g" if i > 1 else "y", "st3" if i > 1 else "st1", "xq", "", T.osc[4 * i:4 * i + 4, :], T.xs[32 * i:32 * i + 4, :], 1024)
+    move("", "yb ps%d" % MARKS, T.yb[:], pm, P, "e")
+    dma("s", "st2", "otb", "", T.ot[:], T.otb[0:128:16, :], 8192)
+    dma("s", "st2", "yb", "", T.y[:], T.yb[:], 131072)
+    return nodes
+
+
+def rank_program(g, core, T, topo):
+    if T.rank_of(core) is None:
+        return
+    nodes = calls(g, core, T, topo)
+    queue = {"v": g.vector, "s": g.scalar, "p": g.tensor, "g": g, "y": g.sync}
+    total, seen, event = {}, {}, {}
+
+    def need(q, s, v):
+        if seen.get((q, s), 0) < v:
+            queue[q].wait_ge(T.sem[s], v)
+            seen[(q, s)] = v
+
+    for i, q in PLAN:
+        nd = nodes[i]
+        if nd["arrival"]:
+            event[i] = nd["arrival"]
+            total[event[i][0]] = event[i][1]
+            continue
+        want = {}
+        for j in nd["deps"]:
+            if event[j]:
+                want[event[j][0]] = max(want.get(event[j][0], 0), event[j][1])
+        for s in sorted(want):
+            need(q, s, want[s])
+        ins = nd["alts"][q][0](queue[q])
+        s = nd["sem"] or "c" + q
+        total[s] = total.get(s, 0) + nd["inc"]
+        if s == "sent":
+            event[i] = None
+        else:
+            ins.then_inc(T.sem[s], nd["inc"])
+            event[i] = (s, total[s])
+    for s in sorted(total):
+        need("g", s, total[s])

@@ -3,84 +3,110 @@ from concourse.mybir import dt, AluOpType as OP, ActivationFunctionType as AF
 
 MC, P, A, K, R = 768, 256, 192, 32, 3
 CODE, U8, U16, BF, F32, I32 = "float8_e4m3fn_x4", "uint8", "uint16", "bfloat16", "float32", "int32"
-XB = [36, 36, 204]
-DB = [3, 3, 11]
-XW = P + A + K
-HZ = XW - P
-SPLIT = [8, 8, 8]
+XC, DC = A, A + P
+ZC = [DC + K, DC + K, DC + A]
+AX = [A + K, A, A]
+AW = [MC + K, MC + 2 * K + A, MC + 2 * K + 2 * A]
+PV = P - 1 - K
+SH = 1024
+UNIT, LIFT = 2.0 ** 70, 2.0 ** 30
+SPLIT = [10, 10, 10]
 ORDER = """
-0y 1s 2y 3s 4y 5y 6y 7g 10v 9g 15v 12s 11v 21s 13v 14v 26v 25v 16v 57v 32s 20s 53v 66s 17g 52v 55v 35g 54v 34s 56v 58g 64v 65s 106v 28s 78v 79s 24v
-80v 67v 84v 27s 33s 107p 108v 19s 83s 18g 85v 86s 110v 87s 109v 144s 135s 8g 22v 153s 88v 23v 145s 150s 89v 180v 90v 136s 46g 138s 151s 141s 81v 152s
-91v 82v 36g 29s 143s 92v 96g 30s 168v 147s 174v 159v 166v 119v 139s 155s 140s 156s 137s 169v 154s 163v 165v 148s 162v 158s 38g 185s 59x 160v 171v 63s
-172v 61s 69v 173v 51v 161v 50v 182v 120v 170v 181v 175v 45g 60s 37g 167v 62s 39g 72s 184s 188v 178v 97x 177v 183v 142s 98s 146s 99v 164v 190v 100g
-101x 179v 157s 186v 149s 75s 176v 191v 193v 192v 187v 40g 94s 194v 195v 197s 121v 49v 115p 31s 198v 199v 210s 208v 209v 47v 211v 309s 68s 43g 212v
-122v 111p 213v 214v 216s 48v 244v 215s 218v 217v 219v 220v 189v 221v 102g 224g 196v 117p 116s 112s 118s 71v 104y 113p 114s 310s 42g 123s 124s 125v
-127p 312v 204v 74s 245v 126p 311v 246v 129p 133v 206v 131s 200v 313v 130s 128p 132s 134s 207s 247v 202v 225x 226v 227v 205s 203s 73s 76s 201v 231v
-314v 70s 95s 232p 233v 235v 234v 293v 281s 288v 294v 287v 228g 272s 278s 263s 260s 307v 296v 229g 230x 240p 269s 280s 264s 242p 308v 261s 300v 284v
-77v 265s 285v 290v 291v 299v 305v 315v 297v 266s 301v 306v 279s 303v 302v 286v 271s 274s 273s 298v 283s 241v 243v 267s 238p 239v 236p 268s 237v 103x
-105v 248v 262s 353p 275s 249s 292v 270s 250v 295v 251p 252p 289v 282s 304v 223v 277s 253p 276s 316v 359p 254p 318v 317v 319v 255s 222v 320v 357p 322v
-256s 321v 323v 331v 324v 329v 333v 257s 325v 258s 259s 330s 334v 327v 332s 326s 336v 328s 44g 337v 348v 41g 354s 338v 335s 355p 339v 356s 349p 350v
-341s 430v 428s 351v 352v 361s 362v 429s 340s 343v 397s 93s 342v 391s 382s 363v 403v 432v 400s 385s 364v 421v 394s 383s 416v 409v 404v 344v 398s 424v
-396s 393s 388s 401s 365v 406v 418v 379s 380s 426v 366v 422v 415v 360s 358s 419v 367v 402s 431v 345v 407v 427v 413v 405v 399s 417v 389s 368s 386s 369v
-410v 373p 346v 434v 420v 371p 392s 408v 412v 411v 425v 423v 384s 381s 414v 395s 387s 390s 435v 437v 436v 433v 370p 438v 439v 372p 440v 446v 450v 444v
-375s 448v 377s 376s 374s 378s 447v 451s 449s 445v 452v 459g 347s 453p 460s 462s 441v 457y 442v 455y 443v 454v 458g 456y 461s
+0y 8g 19v 1y 3s 2y 15v 7y 4s 9g 36s 5y 56v 16v 13g 37v 55v 23v 21v 11g 64v 22v 20v 71v 24v 61v 75v 33s 25s 30s 29s 72v
+76s 10g 31v 46v 86v 45v 47v 70v 77s 12g 107v 38v 57g 42s 52s 108v 110s 109s 39v 88v 17g 133v 40v 35s 87s 111v 78v 113s 134p 28s 112s 114v
+26s 53s 32s 135v 103s 115v 41v 116g 136v 137v 192s 80v 85s 174v 186v 204s 162v 165v 184v 194s 171v 169v 172v 34s 73g 195s 178v 43s 63g 175v 201s 117x
+58v 207s 104v 18g 197s 118v 74x 198s 211v 163v 196s 209v 105s 202s 193s 119v 168v 166v 122s 187v 177v 44s 190v 200s 208s 123v 124g 125x 183v 203s 82v 205s
+79s 60g 65g 199s 210v 106v 126s 167v 189v 6s 83s 180v 173v 188v 181v 179v 121s 191v 176v 120s 212v 182v 14g 206s 170v 185v 214v 164v 62g 127v 213v 215v
+94v 128s 67v 140p 216v 69v 84s 217v 66v 218v 129v 146v 227s 130v 68v 144p 142p 92v 225v 48v 231v 49s 147v 138p 232v 143s 148v 145s 141s 139v 233s 219v
+223v 150v 149s 151v 234s 235v 262v 152p 236s 237v 90v 154p 238v 328v 156s 50v 155p 239v 240g 242v 158s 263v 131v 89v 96v 264v 159v 153p 157s 228v 132v 93s
+160v 241x 95s 243v 221v 224v 226s 220v 222s 244s 249v 245s 265v 91s 27v 250p 246v 247g 229v 230v 161s 266v 97s 251v 252v 81s 253v 98v 321s 326v 300v 101g
+102x 324s 309s 298v 315s 289v 307v 327v 59g 310s 304v 248x 258p 51s 318s 295v 291v 306v 312s 279v 54v 283v 320s 325s 329v 294v 316s 282v 297v 280v 323s 322s
+288v 292v 319s 260p 286v 314s 313s 293v 256p 308v 301v 259s 254p 261s 284v 303v 257s 285v 311s 296v 331v 255s 290v 317s 302v 287v 268s 299v 305v 281v 332v 330v
+333v 267s 334v 335v 336v 340v 344s 269v 271p 345v 272p 342v 338v 275s 346v 347v 270p 276s 348v 349v 273p 274s 350v 351v 277s 99g 100x 368p 278s 366p 343s 370p
+337v 364p 339s 372v 373v 341s 371s 352s 359v 360p 367s 374v 365v 353s 375v 376v 369s 354v 361v 378s 362v 363v 356v 355s 377s 395v 407v 408v 389v 392v 436v 422s
+434s 379v 396v 409v 431s 390v 428s 413v 437v 404v 425s 429s 424s 393v 399v 419s 426s 433s 410v 402v 423s 401v 391v 411v 421s 427s 382p 383p 435s 381p 417v 414v
+416v 397v 432s 412v 405v 420s 403v 394v 398v 418v 439v 415v 430s 400v 385s 406v 441v 386s 438v 440v 380p 384s 442v 357v 387s 443v 358v 444v 388s 452v 453s 446v
+448v 449s 450v 447v 451v 454v 460s 455p 445v 459y 462s 461y 456v 458y 463s 464y 457y
 """
-PLAN = [(int(w[:-1]), w[-1]) for w in ORDER.split()]
-PER_ROUND = {"jm": (P, F32), "jd": (P, F32), "oj": (16, U16), "hm": (P, F32), "m2": (P, F32), "pv": (P, F32), "kk": (P, F32),
-             "nm": (A, BF), "c2": (A, BF), "sj": (2 * A, BF), "js": (2, F32), "jo": (4, U16), "gm": (64, F32), "gs": (64, F32), "ls": (16, U16),
-             "s3": (A, BF), "s4": (A, BF), "s5": (A, BF), "zo": (48, U16), "eqd": (P, BF), "cor": (P, BF), "ra": (16, F32), "gb": (16, F32),
-             "d": (16 * 12, F32), "th": (2, F32), "tpf": (16, F32), "tpu": (16, U16), "xo": (64, U16), "inv": (MC, F32), "zz": (4 * A, BF)}
-
-
-def _sb(n, d):
-    return ("sbuf", [128, n], d)
-
-
-SCRATCH = {
-    "tg32": _sb(16, I32), "ad32": _sb(36, I32), "tgu": _sb(16, U16), "adu": _sb(36, U16),
-    "l2s": _sb(48, U16), "l2r": _sb(48, U16), "lr0": _sb(8, U16), "lr1": _sb(8, U16),
-    "mt": _sb(4 * MC, BF), "ft": _sb(4 * 256, BF), "fq": _sb(224, CODE), "fs": _sb(224, U8), "f1q": _sb(128, CODE), "f1s": _sb(128, U8),
-    "lq": _sb(384, CODE), "lsn": _sb(384, U8), "zt": _sb(512, BF),
-    "strip": _sb(528, BF), "eq": _sb(512, CODE), "es": _sb(512, U8),
-    "ut": _sb(512, BF), "vt": _sb(512, BF), "uq0": _sb(128, CODE), "us0": _sb(128, U8), "uq": _sb(128, CODE), "us": _sb(128, U8),
-    "vq": _sb(128, CODE), "vs": _sb(128, U8), "uoff": _sb(8, U16), "wq": _sb(512, CODE), "wsn": _sb(512, U8),
-    "xt0": _sb(4 * (XB[0] + XW), BF), "xt1": _sb(4 * (XB[1] + XW), BF), "xt2": _sb(4 * (XB[2] + XW), BF), "xt3": _sb(4 * P, BF),
-    "xq": _sb(P, CODE), "xs": _sb(P, U8), "zq": _sb(A, CODE), "zs": _sb(A, U8),
-    "iot": _sb(MC, F32), "ones": _sb(MC, BF), "at0": _sb(MC, BF), "acc0": _sb(208, BF), "acc1": _sb(976, BF), "acc2": _sb(976, BF),
-    "n33": _sb(A, BF), "prow": _sb(P, BF), "jrow": _sb(A, BF), "s1": _sb(A, BF), "s2": _sb(A, BF),
-    "pat16": _sb(P, BF), "pat4": _sb(A, BF), "mask16": _sb(P, BF), "keep16": _sb(P, BF), "c16": _sb(P, BF), "r16": _sb(P, BF),
-    "mask4": _sb(A, BF), "keep4": _sb(A, BF),
-    "pi": _sb(4, I32), "pj": _sb(4, I32), "pc": _sb(8, F32), "kc": _sb(2, F32), "pd": _sb(16, F32), "pdm": _sb(16, F32), "cb": _sb(48, F32),
-    "jw1": _sb(288, F32), "jw2": _sb(320, F32), "ir01": _sb(A, F32), "ir02": _sb(A, F32), "ir12": _sb(A, F32),
-    "tw": _sb(352, F32), "aw": _sb(4 * A, F32), "cmp": _sb(16 * P, BF), "cnt": _sb(16 * 128, BF),
-    "yb": _sb(P, F32), "otb": _sb(P, F32),
-    "ps": ("psum", [128, 4096], F32),
+PER_ROUND = {"jl": (P, F32), "xx": (16, F32), "nm": (A + K, BF), "sj": (2 * (A + K), BF), "js": (2, F32),
+             "jo": (2, U16), "gs": (64, F32), "lst": (16, U16), "al": (K, F32), "alu": (2, U16), "zl": (2 * A + K, BF), "zm": (4 * 48, F32), "zo": (48, U16),
+             "zz": (4 * A, BF), "m2": (P, F32), "pv": (P, F32), "kk": (P, F32), "eqd": (P, BF), "cor": (P, BF), "ra": (16, F32), "gb": (16, F32),
+             "e1": (16, F32), "e2": (16, F32), "th": (2, F32), "tpu": (16, U16), "xo": (64, U16), "k16": (P, BF)}
+WIDTH = {
+    "tg32": (16, I32), "ad32": (36, I32), "tgu": (16, U16), "adu": (36, U16), "lr": (16, U16), "l2r": (16, U16), "l2o": (48, U16),
+    "mt": (4 * (MC + K), BF), "ft": (640, BF), "ft2": (4 * A, BF), "fq": (256 + A, CODE), "fs": (256 + A, U8),
+    "lq": (192 + A, CODE), "lsn": (384 + A, U8), "zt": (512, BF),
+    "ones": (528, BF), "strip": (528, BF), "eq": (512, CODE), "es": (512, U8),
+    "ut": (512, BF), "vt": (512, BF), "uq0": (128, CODE), "us0": (128, U8), "uq": (128, CODE), "us": (128, U8),
+    "vq": (128, CODE), "vs": (128, U8), "uoff": (8, U16), "wq": (512, CODE), "wsn": (512, U8),
+    "xt0": (4 * (ZC[0] + 4), BF), "xt1": (4 * (ZC[1] + K), BF), "xt2": (4 * (ZC[2] + 4), BF), "xt3": (4 * P, BF),
+    "xq": (P, CODE), "xs": (P, U8), "zq": (A, CODE), "zs": (A, U8),
+    "iot": (AW[2] + A, F32), "inv": (R * MC + K, F32), "at0": (MC + K, BF), "cap": (A + K, BF), "prow": (K + P, BF), "yrow": (P, F32),
+    "ca0": (2 * A + K, BF), "ca1": (2 * A, BF), "ca2": (A + DC, BF), "oj": (16, U16),
+    "jd0": (P, F32), "jd1": (P + 2 * K + 8, F32), "jd2": (P, F32), "v1": (A, BF), "v16": (A, BF), "v4": (A, BF), "v4m": (48, F32), "pl": (12, U16), "j4": (48, F32),
+    "pat16": (P, BF), "pat4": (2 * A + K, BF), "sa": (P, BF), "sb": (P, BF), "sel16": (P, BF), "sel4": (2 * A + K, BF), "c16": (P, BF), "r16": (P, BF),
+    "pi": (4, I32), "pj": (4, I32), "pc": (24, F32), "t4": (16, F32), "pd": (16, F32), "ds": (48 * (R + 1), F32), "d0": (48, F32),
+    "jw1": (P + K, F32), "jw2": (P + 2 * K, F32), "tw": (P + 4 * K, F32), "cmp": (16 * P, BF), "cnt": (16 * 128, BF),
+    "yb": (P, F32), "otb": (P, F32), "ps": (4096, F32),
 }
 for _n in PER_ROUND:
-    SCRATCH[_n] = _sb(R * PER_ROUND[_n][0], PER_ROUND[_n][1])
+    WIDTH[_n] = (R * PER_ROUND[_n][0], PER_ROUND[_n][1])
+SCRATCH = {_n: ("psum" if _n == "ps" else "sbuf", [128, WIDTH[_n][0]], WIDTH[_n][1]) for _n in WIDTH}
 LOADS = ["tg", "ad", "x", "u", "m", "wc", "ws", "v"]
-SEMAPHORES = ["cv", "cs", "cp", "cg", "sent", "a_l2", "a_l0", "a_l1", "a_f0", "a_f2", "a_f1", "st1", "st2", "st3"] + ["ld_" + n for n in LOADS]
+SEMAPHORES = ["cv", "cs", "cp", "cg", "sent", "st", "a_l0", "a_l1", "a_l2", "a_f0", "a_f1", "a_f2", "a_s2"] + ["ld_" + n for n in LOADS]
 
 
-def calls(g, core, T, topo):
+def W(name, a=0, b=None, step=1):
+    return (name, a, WIDTH[name][0] if b is None else b, step)
+
+
+def B(name, t, a=0, b=None, step=1):
+    w = PER_ROUND[name][0]
+    return (name, w * t + a, w * t + (w if b is None else b), step)
+
+
+def IND(win, off):
+    return ("@", win, off)
+
+
+def RAW(view, d):
+    return ("#", view, d)
+
+
+def calls(core, T, topo):
     rank, n = T.rank_of(core), len(T.cores)
     owner, asker = T.cores[(rank + 1) % n], T.cores[(rank - 1) % n]
-    nodes, wrote, read = [], {}, {}
+    nodes, touched = [], {}
 
-    def node(rd, wr, alts, sem=None, inc=1, arrival=None):
-        rd, wr = rd.split(), wr.split()
-        deps = set(wrote[k] for k in rd if k in wrote)
-        for k in wr:
-            deps |= set(read.get(k, []))
-            if k in wrote:
-                deps.add(wrote[k])
-        i = len(nodes)
-        nodes.append({"deps": sorted(deps), "alts": alts, "sem": sem, "inc": inc, "arrival": arrival})
-        for k in rd:
-            read.setdefault(k, []).append(i)
-        for k in wr:
-            wrote[k] = i
-            read[k] = []
+    def ap(x):
+        if not isinstance(x, tuple):
+            return x
+        if x[0] == "@":
+            return ap(x[1]).indirect(ap(x[2]))
+        if x[0] == "#":
+            return ap(x[1]).bitcast(x[2])
+        return T[x[0]][:, x[1]:x[2]] if x[3] == 1 else T[x[0]][:, x[1]:x[2]:x[3]]
+
+    def plain(xs):
+        o = []
+        for x in xs:
+            if isinstance(x, tuple):
+                o += plain(x[1:]) if x[0] in "@#" else [x]
+        return o
+
+    def node(rd, wr, alts, tag="", sem=None, inc=1, arrival=None, after=()):
+        rd = plain(rd) + plain([x[2] for x in wr if x[0] == "@"])
+        wr = plain([x[1] if x[0] == "@" else x for x in wr])
+        deps, i = set(after), len(nodes)
+        for views, writes in ((rd, False), (wr, True)):
+            for name, a, b, s in views:
+                m = ((1 << (b - a)) - 1) << a if s == 1 else sum(1 << e for e in range(a, b, s))
+                log = touched.setdefault(name, [])
+                deps |= set(j for j, m2, w in log if m2 & m and (w or writes) and j != i)
+                if writes:
+                    log[:] = [(j, m2 & ~m, w) for j, m2, w in log if m2 & ~m]
+                log.append((i, m, writes))
+        nodes.append({"deps": sorted(deps), "alts": alts, "sem": sem, "inc": inc, "arrival": arrival, "tag": tag or (wr[0][0] if wr else "")})
         return i
 
     def lanes(src, dst):
@@ -89,324 +115,343 @@ def calls(g, core, T, topo):
     def bits(es):
         return sum(1 << e for e in es)
 
-    def send(dst, src, sem, rd, lands, size, pairs, before=0):
+    def send(dst, src, sem, pairs):
         rid, pid = topo.addr(dst, core)
         es = lanes(core, dst)
 
         def f(e):
             if len(pairs) == 1:
-                return e.remote_dma(pairs[0][0], pairs[0][1], T.sem[sem], T.sem.sent, pid, rid, bits(es))
+                return e.remote_dma(ap(pairs[0][0]), ap(pairs[0][1]), T.sem[sem], T.sem.sent, pid, rid, bits(es))
             h = len(es) // 2
             return e.remote_dma_fused([RemoteDMATransfer(dst_ids=[DstId(rid=rid, pnc=pid)], dma_engine_mask=bits(es[h * i:h * i + h]), remote_sem=T.sem[sem],
-                                                         src=pairs[i][1], dst=pairs[i][0]) for i in range(2)], local_sem=T.sem.sent)
-        node(rd + " wire", "wire sent_" + sem, {"g": (f, "send", size)}, sem="sent", inc=len(es))
-        if lands:
-            node("sent_" + sem, lands, {"x": (None, "far", size)}, arrival=(sem, (1 + before) * len(lanes(src, core))))
+                                                         src=ap(pairs[i][1]), dst=ap(pairs[i][0])) for i in range(2)], local_sem=T.sem.sent)
+        i = node([p[1] for p in pairs], [], {"g": f}, "send " + sem, sem="sent", inc=len(es))
+        node([], [p[0] for p in pairs], {"x": None}, sem, arrival=(sem, len(lanes(src, core))), after=[i])
 
-    def V(rd, wr, f, kind, size):
-        node(rd, wr, {"v": (f, kind, size)})
-
-    def ts(rd, wr, out, a, s1, o1, s2=None, o2=None, c=64):
+    def ts(out, a, s1, o1, s2=None, o2=None):
         if s2 is None:
-            V(rd, wr, lambda e: e.tensor_scalar(out, a, s1, None, o1), "e", c)
+            node([a, s1], [out], {"v": lambda e: e.tensor_scalar(ap(out), ap(a), ap(s1), None, o1)})
         else:
-            V(rd, wr, lambda e: e.tensor_scalar(out, a, s1, s2, o1, o2), "e", c)
+            node([a, s1, s2], [out], {"v": lambda e: e.tensor_scalar(ap(out), ap(a), ap(s1), ap(s2), o1, o2)})
 
-    def tt(rd, wr, out, a, b, o, c=64, kind="e"):
-        V(rd, wr, lambda e: e.tensor_tensor(out, a, b, o), kind, c)
+    def tt(out, a, b, o):
+        node([a, b], [out], {"v": lambda e: e.tensor_tensor(ap(out), ap(a), ap(b), o)})
 
-    def cp(rd, wr, out, a, c=64, kind="e"):
-        V(rd, wr, lambda e: e.tensor_copy(out, a), kind, c)
+    def cp(out, a):
+        node([a], [out], {"v": lambda e: e.tensor_copy(ap(out), ap(a))})
 
-    def scan(rd, wr, out, a, b, init, o0, o1, c):
-        V(rd, wr, lambda e: e.tensor_tensor_scan(out, a, b, init, o0, o1), "e", c)
+    def scan(out, a, b, init, o0, o1):
+        node([a, b], [out], {"v": lambda e: e.tensor_tensor_scan(ap(out), ap(a), ap(b), init, o0, o1)})
 
-    def quant(rd, wr, q, s, a, cols):
-        V(rd, wr, lambda e: e.quantize_mx(q, s, a), "q", 4 * cols)
+    def quant(q, s, a):
+        node([a], [q, s], {"v": lambda e: e.quantize_mx(ap(q), ap(s), ap(a))})
 
-    def act(rd, wr, out, a, f, c=64, kind="e", **kw):
-        node(rd, wr, {"s": (lambda e: e.activation(out, a, f, **kw), kind, c)})
+    def act(out, a, f, scale=1.0, bias=0.0, total=None):
+        if total is None:
+            node([a, scale, bias], [out], {"s": lambda e: e.activation(ap(out), ap(a), f, scale=ap(scale), bias=ap(bias))})
+        else:
+            node([a, scale, bias], [out, total], {"s": lambda e: e.activation(ap(out), ap(a), f, scale=ap(scale), bias=ap(bias), accum_out=ap(total))})
 
-    def move(rd, wr, out, a, c, kind="ga"):
-        node(rd, wr, {"s": (lambda e: e.activation(out, a, AF.Copy), kind, c), "v": (lambda e: e.tensor_copy(out, a), kind, c)})
+    def move(out, a):
+        node([a], [out], {"s": lambda e: e.activation(ap(out), ap(a), AF.Copy), "v": lambda e: e.tensor_copy(ap(out), ap(a))})
 
-    def lin(rd, wr, out, a, scale, bias, c=64):
-        node(rd, wr, {"s": (lambda e: e.activation(out, a, AF.Identity, scale=scale, bias=bias), "e", c),
-                      "v": (lambda e: e.tensor_scalar(out, a, scale, bias, OP.mult, OP.add), "e", c)})
+    def lin(out, a, scale, bias):
+        node([a, scale, bias], [out], {"s": lambda e: e.activation(ap(out), ap(a), AF.Identity, scale=ap(scale), bias=ap(bias)),
+                                       "v": lambda e: e.tensor_scalar(ap(out), ap(a), ap(scale), ap(bias), OP.mult, OP.add)})
 
-    def steps(wr, out, width, base, step=0, only=None):
-        alts = {"g": (lambda e: e.iota(out, [[step, width]], base, 0, allow_small_or_imprecise_dtypes=True), "g", width)}
-        if step == 0:
-            alts["v"] = (lambda e: e.memset(out, float(base)), "e", width // 2)
-        if only:
-            alts = {only: alts[only]}
-        node("", wr, alts)
+    def steps(out, pattern, base):
+        node([], [out], {"g": lambda e: e.iota(ap(out), pattern, base, 0, allow_small_or_imprecise_dtypes=True)})
 
-    def mm(rd, bank, w, ws, x, xs, cols):
-        node(rd, "ps%d" % bank, {"p": (lambda e: e.matmul_mx(T.ps[:, 512 * bank:512 * bank + cols], w, ws, x, xs, True, True), "mm", cols)})
+    def fill(out, c):
+        node([], [out], {"g": lambda e: e.iota(ap(out), [[0, out[2] - out[1]]], c, 0, allow_small_or_imprecise_dtypes=True),
+                         "v": lambda e: e.memset(ap(out), float(c))})
 
-    def dma(q, sem, rd, wr, out, a, size):
-        node(rd, wr, {q: (lambda e: e.dma_start(out, a), "dma", size)}, sem=sem, inc=16)
+    def bank(b, a=0, w=512):
+        return W("ps", 512 * b + a, 512 * b + a + w)
 
-    def B(name, t, a=0, b=None, step=1):
-        w = PER_ROUND[name][0]
-        return T[name][:, w * t + a:w * t + (w if b is None else b):step]
+    def mm(b, w, ws, x, xs):
+        node([w, ws, x, xs], [bank(b)], {"p": lambda e: e.matmul_mx(ap(bank(b, 0, x[2] - x[1])), ap(w), ap(ws), ap(x), ap(xs), True, True)})
 
-    xt = [T.xt0, T.xt1, T.xt2, T.xt3]
-    acc = [T.acc0[:, 0:A], T.acc1[:, 1:A + 1], T.acc2[:, 1:A + 1]]
-    jw = [None, T.jw1, T.jw2]
-    adu = [T.adu[:, 12 * t:12 * t + 12] for t in range(R)]
-    xbase = [4 * XB[0], 4 * XB[1], 4 * XB[2], 0]
-    MARKS = 0
-    pm = T.ps[:, 512 * MARKS:512 * MARKS + P]
+    def dma(sem, rd, wr, out, a):
+        node(rd, wr, {"y": lambda e: e.dma_start(out, a), "s": lambda e: e.dma_start(out, a)}, sem, sem=sem, inc=16)
 
-    dma("y", "ld_tg", "q1", "q1 tg32", T.tg32[:], T.tg[:], 8192)
-    dma("s", "ld_ad", "", "ad32", T.ad32[:], T.ad[:], 18432)
-    dma("y", "ld_x", "", "X0", T.xt0[:, xbase[0]:xbase[0] + 4 * P], T.x[:], 280000)
-    dma("s", "ld_u", "", "ut", T.ut[:], T.u[:], 420000)
-    dma("y", "ld_m", "", "mt", T.mt[:], T.m[:], 1200000)
-    dma("y", "ld_wc", "", "wq", T.wq[:].bitcast(dt.uint8), T.wc[:], 1460000)
-    dma("y", "ld_ws", "", "wsn", T.wsn[:], T.ws[:], 1530000)
+    def load(name, view):
+        dma("ld_" + name, [], [view], ap(view), T[name][:])
 
-    node("", "pi", {"g": (lambda e: e.iota(T.pi[:, 0:1], [[0, 1]], 0, 1), "g", 1)})
-    node("", "pat4", {"g": (lambda e: e.iota(T.pat4[:], [[0, A // 4], [1, 4]], 0, 0, allow_small_or_imprecise_dtypes=True), "g", A)})
-    node("", "pat16", {"g": (lambda e: e.iota(T.pat16[:], [[0, 16], [1, 16]], 0, 0, allow_small_or_imprecise_dtypes=True), "g", P)})
-    steps("ones", T.ones[:], MC, 1, only="v")
-    scan("ones", "iot", T.iot[:], T.ones[:], T.ones[:], -1.0, OP.add, OP.mult, MC)
-    lin("ones", "at0", T.at0[:], T.ones[:], 0.0, -64.0, MC)
-    ts("pi", "pj0", T.pj[:, 0:1], T.pi[:, 0:1], 15, OP.bitwise_and)
-    ts("pi", "pj1", T.pj[:, 1:2], T.pi[:, 0:1], 3, OP.bitwise_and)
-    ts("pi", "pj2", T.pj[:, 2:3], T.pi[:, 0:1], 2, OP.logical_shift_right, 3, OP.bitwise_and)
-    cp("pj0 pj1 pj2", "pc", T.pc[:, 0:3], T.pj[:, 0:3])
-    steps("prow", T.prow[:], P, 1, 1)
-    steps("n33", T.n33[:], A, -33)
-    lin("pc", "kc0", T.kc[:, 0:1], T.pc[:, 0:1], -1.0, 31.5)
-    lin("pc", "kc1", T.kc[:, 1:2], T.pc[:, 0:1], -1.0, 15.5)
-    move("iot", "awi", T.aw[:, 0:A], T.iot[:, 0:A], A, "e")
-    ts("pc pat4", "mask4", T.mask4[:], T.pat4[:], T.pc[:, 2:3], OP.is_equal, c=96)
-    ts("pat4", "keep4", T.keep4[:], T.pat4[:], 0.0, OP.not_equal, c=96)
-    ts("pc pat16", "mask16", T.mask16[:], T.pat16[:], T.pc[:, 0:1], OP.is_equal, c=128)
-    ts("pat16", "keep16", T.keep16[:], T.pat16[:], 0.0, OP.not_equal, c=128)
-    cp("iot", "uoff", T.uoff[:], T.iot[:, 0:128:16])
-    lin("mask16", "c16", T.c16[:], T.mask16[:], -9e29, 4.5e29, P)
-    lin("keep16", "r16", T.r16[:], T.keep16[:], -9e29, 4.5e29, P)
-    lin("iot pc", "pd", T.pd[:], T.iot[:, 0:P:16], 1.0, T.pc[:, 0:1])
-    lin("pd", "pdm", T.pdm[:], T.pd[:], 1.0, -255.0)
-    lin("pc", "zc0", T.pc[:, 4:5], T.pc[:, 1:2], 1.0, 4.0 * (XB[0] - 1))
-    lin("pc", "zc2", T.pc[:, 5:6], T.pc[:, 1:2], 1.0, 4.0 * (XB[2] - 1))
-    for a in sorted(set(SPLIT)):
-        o = 16 * SPLIT.index(a)
-        lin("iot", "cbs%d" % a, T.cb[:, o:o + a], T.iot[:, 0:a], -16.0, float(HZ - 16))
-        lin("iot", "cbv%d" % a, T.cb[:, o + a:o + 16], T.iot[:, a:16], 0.0, float(HZ))
+    def pc(i):
+        return W("pc", i, i + 1)
+
+    def X(t):
+        return W("xt%d" % t, 4 * XC, 4 * DC) if t < R else W("xt3")
+
+    def DS(t, e=0, a=0, b=16):
+        return W("ds", 48 * t + 3 * a + e, 48 * t + 3 * b, 3)
+
+    def INV(t, more=0):
+        return W("inv", MC * t, MC * t + MC + more)
+
+    def bytes_of(name, a, b):
+        return RAW(W(name, a, b), dt.uint8)
+
+    pm = bank(0, 0, P)
+    adu = [W("adu", 12 * t, 12 * t + 12) for t in range(R)]
+    places = W("prow", K)
+    jd = [W("jd0"), W("jd1", K, K + P), W("jd2")]
+
+    load("tg", W("tg32"))
+    load("ad", W("ad32"))
+    load("x", X(0))
+    load("u", W("ut"))
+    load("m", W("mt", 0, 4 * MC))
+    load("wc", RAW(W("wq"), dt.uint8))
+    load("ws", W("wsn"))
+    load("v", W("vt"))
+
+    node([], [W("pi", 0, 1)], {"g": lambda e: e.iota(ap(W("pi", 0, 1)), [[0, 1]], 0, 1)})
+    steps(W("prow"), [[1, K + P]], 1 - P)
+    steps(W("pat16"), [[0, 16], [1, 16]], 0)
+    steps(W("iot", 0, MC + K), [[1, MC + K]], 0)
+    steps(W("iot", AW[0] + A, AW[1]), [[1, K]], MC)
+    steps(W("pat4"), [[0, (2 * A + K) // 4], [1, 4]], 0)
+    steps(W("d0"), [[0, 16], [30000, 3]], -30000)
+    fill(W("at0"), 2 * K + 1)
+    fill(INV(0), 0)
+    fill(INV(1), 0)
+    fill(INV(2, K), 0)
+    fill(W("cap"), 2 * K + 1)
+    fill(B("nm", 0, A), 1)
+    ts(W("pj", 0, 1), W("pi", 0, 1), 15, OP.bitwise_and)
+    ts(W("pj", 1, 2), W("pi", 0, 1), 3, OP.bitwise_and)
+    ts(W("pj", 2, 3), W("pi", 0, 1), 2, OP.logical_shift_right, 3, OP.bitwise_and)
+    cp(W("pc", 0, 3), W("pj", 0, 3))
+    lin(pc(3), pc(0), 1.0, 1.0)
+    lin(pc(4), pc(1), 1.0, 4.0 * PV + 0.25)
+    lin(pc(10), pc(1), 1.0, 4.0 * (PV + K) + 0.25)
+    lin(pc(5), pc(1), 1.0, 0.25)
+    lin(pc(6), pc(0), 1.0, K + 0.5)
+    lin(pc(7), pc(0), 1.0, K + 16.5)
+    ts(pc(9), pc(0), 15.0, OP.is_equal, 1.0 / LIFT, OP.max)
+    lin(pc(8), pc(9), -1.0 / UNIT, 0.0)
+    lin(pc(11), pc(0), 1.0, float(XC - SH + PV))
+    lin(W("pd"), W("prow", K, K + P, 16), 1.0, pc(11))
+    lin(DS(0, 2), W("prow", K, K + P, 16), 1.0, pc(11))
+    lin(W("yrow"), places, -UNIT, (2 * SH - DC - PV) * UNIT)
+    ts(W("uoff"), W("prow", K, K + 128, 16), float(PV), OP.add)
+    ts(W("c16"), W("pat16"), pc(0), OP.not_equal, 2.0 ** 90, OP.mult)
+    ts(W("sa"), W("pat16"), pc(0), OP.not_equal)
+    ts(W("sb"), W("pat16"), pc(3), OP.is_equal, LIFT, OP.mult)
+    tt(W("sel16"), W("sa"), W("sb"), OP.max)
+    lin(W("r16"), W("pat16"), -2.0 ** 96, 2.0 ** 95)
+    k16 = []
     for t in range(R):
-        steps("inv%d" % t, B("inv", t), MC, A + 1, 1)
-    steps("zt", T.zt[:], 512, 0)
-    steps("D0", T.xt0[:, 0:xbase[0]], xbase[0], 0)
-    steps("D1", T.xt1[:, 0:xbase[1]], xbase[1], 0)
-    steps("D2", T.xt2[:, 0:4 * DB[2]], 4 * DB[2], 0)
-    steps("D2z", T.xt2[:, xbase[2] - 4:xbase[2]], 4, 0)
-    steps("acc1", acc[1], A, -64)
-    steps("acc2", acc[2], A, -512)
-    steps("jrow", T.jrow[:], A, -A, 1)
-    node("ones", "strip", {"g": (lambda e: e.affine_select(T.strip[:], T.ones[:, 0:528], [[1, 528]], OP.is_equal, 0.0, -3, -4), "g", 550)})
+        a, o = SPLIT[t], SPLIT.index(SPLIT[t])
+        k16.append(B("k16", o))
+        if o == t:
+            lin(B("k16", t), W("pat16"), 512.0, 0.0)
+            if a < 16:
+                lin(B("k16", t, 16 * a, P, 16), W("prow", K + 16 * a, K + P, 16), -1.0, float(-PV - 16))
+    ts(W("sel4"), W("pat4"), pc(2), OP.is_gt, 2.0 ** 20, OP.mult)
+    ts(W("t4", 0, 4), W("pat4", 0, 4), pc(2), OP.is_le, 2.0 ** -10, OP.max)
+    scan(W("t4", 4, 8), W("t4", 0, 4), W("t4", 0, 4), 4.0, OP.mult, OP.mult)
+    sc4 = W("t4", 7, 8)
+    node([sc4], [pc(12)], {"v": lambda e: e.reciprocal(ap(pc(12)), ap(sc4))})
+    lin(pc(13), pc(12), 4.0 * K, 0.0)
+    lin(pc(14), pc(12), -2000.0, 0.0)
+    lin(pc(15), pc(12), 4.0 * (2 * K + 0.5), 0.0)
+    lin(pc(16), pc(2), 1.0, K + 1.0)
+    lin(W("j4"), W("iot", 0, A, 4), 1.0, pc(16))
+    ts(W("j4"), W("j4"), pc(12), OP.mult, 4.0, OP.mult)
+    fill(W("zt"), 0)
+    fill(W("ft", 128, 512), 0)
+    fill(W("mt", 4 * MC), 0)
+    for t in range(R):
+        fill(W("xt%d" % t, 4 * ZC[t], 4 * ZC[t] + 16), 0)
+    fill(W("ra"), 0)
+    fill(W("jd1", K + P), 0)
+    fill(W("ca2", A, 2 * A), K + 1 + A)
+    fill(W("ones"), 1)
+    node([W("ones")], [W("strip")], {"g": lambda e: e.affine_select(ap(W("strip")), ap(W("ones")), [[1, 528]], OP.is_equal, 0.0, -3, -4)})
     for b in range(4):
-        quant("strip", "eq%d" % b, T.eq[:, 128 * b:128 * b + 128], T.es[:, 128 * b:128 * b + 128], T.strip[:, 3 - b:3 - b + 512], 128)
-    quant("zt", "lZ", T.lq[:, 32:160], T.lsn[:, 32:160], T.zt[:], 128)
+        quant(W("eq", 128 * b, 128 * b + 128), W("es", 128 * b, 128 * b + 128), W("strip", 3 - b, 3 - b + 512))
+    quant(W("lq", 32, 160), W("lsn", 128, 256), W("zt"))
 
-    cp("tg32", "tgu", T.tgu[:], T.tg32[:])
-    cp("ad32", "adu", T.adu[:], T.ad32[:])
-    for e in range(4):
-        ts("ad32", "l2s%d" % e, T.l2s[:, 12 * e:12 * e + 12], T.ad32[:, 24:36], 4.0, OP.mult, float(e), OP.add)
-    send(owner, asker, "a_l2", "l2s0 l2s1 l2s2 l2s3", "l2r", 12288, [(T.l2r[:], T.l2s[:])])
-    for e in range(4):
-        move("mt l2r", "F2%d" % e, T.ft[:, 256 + e:1024:4], T.mt[:].indirect(T.l2r[:, 12 * e:12 * e + 12]), A)
-    cp("tgu prow", "at0", T.at0[:].indirect(T.tgu[:]), T.prow[:], P, "sc")
-    move("at0 adu", "acc0", acc[0], T.at0[:].indirect(adu[0]), A)
+    cp(W("tgu"), W("tg32"))
+    cp(W("adu"), W("ad32"))
+    send(owner, asker, "a_l2", [(W("l2r", 0, 12), adu[2])])
+    cp(IND(W("at0"), W("tgu")), places)
+    move(W("ca0", AX[0]), IND(W("at0"), adu[0]))
     for t in range(R):
-        move("iot adu", "aw%d" % t, T.aw[:, A * (t + 1):A * (t + 2)], T.iot[:].indirect(adu[t]), A)
-        cp("iot adu", "inv%d" % t, B("inv", t).indirect(adu[t]), T.iot[:, 1:A + 1], A, "sc")
-    move("inv1 adu", "ir01", T.ir01[:], B("inv", 1).indirect(adu[0]), A)
-    move("inv2 adu", "ir02", T.ir02[:], B("inv", 2).indirect(adu[0]), A)
-    move("inv2 adu", "ir12", T.ir12[:], B("inv", 2).indirect(adu[1]), A)
-    move("inv1 tgu", "jw1a", T.jw1[:, 0:P], B("inv", 1).indirect(T.tgu[:]), P)
-    move("inv2 tgu", "jw2a", T.jw2[:, 0:P], B("inv", 2).indirect(T.tgu[:]), P)
-    move("iot tgu", "twa", T.tw[:, 0:P], T.iot[:].indirect(T.tgu[:]), P)
-    quant("ut", "uq0", T.uq0[:], T.us0[:], T.ut[:], 128)
-    move("uq0 uoff", "us", T.us[:], T.us0[:].indirect(T.uoff[:]), 128)
-    cp("uq0 uoff", "uq", T.uq[:].bitcast(dt.uint32), T.uq0[:].bitcast(dt.uint32).indirect(T.uoff[:]), 128, "ga")
-
-    def unpack(t):
-        a, cols = [(64, 128), (0, 128), (192, 192)][t]
-        o, w = [(96, K), (0, K), (0, A)][t]
-        rd = ["lZ lF0", "lZ lF1", "lF0 lF2"][t]
-        for b in range(4):
-            mm(rd + " eq%d" % b, 4 + b, T.eq[:, 128 * b:128 * b + 128], T.es[:, 128 * b:128 * b + 128], T.lq[:, a:a + cols], T.lsn[:, a:a + cols], cols)
-            e, c = 4 * DB[t], 512 * (4 + b) + o
-            move("D%d" % t, "ps%d D%d%d" % (4 + b, t, b), xt[t][:, e + b:e + 4 * w:4], T.ps[:, c:c + w], w, "e")
+        move(W("iot", AW[t], AW[t] + A), IND(W("iot", 0, MC), adu[t]))
+        cp(IND(INV(t), adu[t]), W("yrow", K * t, K * t + A))
+    move(W("jw1", 0, P), IND(INV(1), W("tgu")))
+    move(W("jw2", 0, P), IND(INV(2), W("tgu")))
+    move(W("tw", 0, P), IND(W("iot", 0, MC), W("tgu")))
+    quant(W("uq0"), W("us0"), W("ut"))
+    move(W("us"), IND(W("us0"), W("uoff")))
+    cp(RAW(W("uq"), dt.uint32), IND(RAW(W("uq0"), dt.uint32), W("uoff")))
+    quant(W("vq"), W("vs"), W("vt"))
+    for e in range(4):
+        ts(W("l2o", 12 * e, 12 * e + 12), W("l2r", 0, 12), 4.0, OP.mult, float(e), OP.add)
+        move(W("ft2", e, 4 * A, 4), IND(W("mt", 0, 4 * MC), W("l2o", 12 * e, 12 * e + 12)))
+    quant(W("fq", 256), W("fs", 256), W("ft2"))
+    send(asker, owner, "a_f2", [(bytes_of("lq", 192, 192 + A), bytes_of("fq", 256, 256 + A))])
+    send(asker, owner, "a_s2", [(W("lsn", 384), W("fs", 256))])
 
     def marks(t):
-        quant("X%d X%d0 X%d1 X%d2 X%d3" % ((t,) * 5), "xq", T.xq[:], T.xs[:], xt[t][:, xbase[t]:xbase[t] + 4 * P], P)
-        if t < 3:
-            mm("xq uq us", MARKS, T.uq[:], T.us[:], T.xq[:], T.xs[:], P)
+        quant(W("xq"), W("xs"), X(t))
+        if t < R:
+            mm(0, W("uq"), W("us"), W("xq"), W("xs"))
         else:
-            mm("xq vq", MARKS, T.vq[:], T.vs[:], T.xq[:], T.xs[:], P)
+            mm(0, W("vq"), W("vs"), W("xq"), W("xs"))
 
     def one_round(t):
-        def k(s):
-            return s.replace("#", str(t))
-
-        def D(i, a=0, b=16):
-            return B("d", t, 16 * i + a, 16 * i + b)
-
-        JD, a = B("jd", t, 15, P, 16), SPLIT[t]
-        if t == 0:
-            rd, src = "inv0 tgu", B("inv", 0).indirect(T.tgu[:])
-        else:
-            rd, src = k("jw#a jw#b jw#c tpu%d" % (t - 1)), jw[t][:].indirect(B("tpu", t - 1))
-        tt(rd + " mask16", k("jm#"), B("jm", t), src, T.mask16[:], OP.mult, P, "ga")
-        scan(k("jm# keep16"), k("jd#"), B("jd", t), T.keep16[:], B("jm", t), 0.0, OP.mult, OP.add, P)
-        act(rd, k("hm#"), B("hm", t), src, AF.Relu, P, "ga", scale=-1e27, bias=192.5e27)
-        if t > 0:
-            cp(k("jd#"), k("oj#"), B("oj", t), JD)
-            cp(k("oj# prow"), k("acc#"), T["acc%d" % t][:].indirect(B("oj", t)), T.prow[:], P, "sc")
-        ts(k("acc#"), k("nm#"), B("nm", t), acc[t], 0.0, OP.is_lt, -1.0, OP.mult, 96)
-        scan(k("nm# n33"), k("c2#"), B("c2", t), B("nm", t), T.n33[:], 0.0, OP.add, OP.max, 96)
-        for i in range(2):
-            act(k("c2# kc%d" % i), k("js#%d" % i), B("sj", t, A * i, A * i + A - 1), B("c2", t, 0, A - 1), AF.Sign, A + 20, bias=T.kc[:, i:i + 1],
-                accum_out=B("js", t, i, i + 1))
-        ts(k("js#0 js#1"), k("joa#"), B("jo", t, 0, 2), B("js", t), 0.5, OP.mult, 95.5 + A * (t + 1), OP.add)
-        ts(k("js#0 js#1"), k("job#"), B("jo", t, 2, 4), B("js", t), 0.5, OP.mult, 95.5, OP.add)
-        rd = "awi " + " ".join("aw%d" % i for i in range(t + 1))
-        tt(rd + k(" joa# job# mask4"), k("gm#"), B("gm", t), T.aw[:, 0:A * (t + 2)].indirect(B("jo", t)), T.mask4[:, 0:64], OP.mult, 64, "ga")
-        scan(k("gm# keep4"), k("gs#"), B("gs", t), T.keep4[:, 0:64], B("gm", t), 0.0, OP.mult, OP.add, 64)
-        ts(k("gs# pc"), k("ls#"), B("ls", t), B("gs", t, 3, 64, 4), 4.0, OP.mult, T.pc[:, 1:2], OP.add)
-        jk = B("jo", t, 2, 4)
-        move(k("aw# job#"), k("tw#"), T.tw[:, P + K * t:P + K * t + K], T.aw[:, A * (t + 1):A * (t + 2)].indirect(jk), K)
-        if t == 0:
-            move("ir01 job0", "jw1b", T.jw1[:, P:P + K], T.ir01[:].indirect(jk), K)
-            move("ir02 job0", "jw2b", T.jw2[:, P:P + K], T.ir02[:].indirect(jk), K)
-            send(owner, asker, "a_l0", "ls0", "lr0", 2048, [(T.lr0[:], B("ls", 0, 0, 8))])
-            move("mt lr0", "F0", T.ft[:, 128:256], T.mt[:].indirect(T.lr0[:]), 128)
-            quant("F0 F20 F21 F22 F23", "fq", T.fq[:], T.fs[:], T.ft[:, 128:1024], 224)
-            send(asker, owner, "a_f0", "fq", "lF0", 57344, [(T.lq[:, 160:216].bitcast(dt.uint8), T.fq[:, 0:56].bitcast(dt.uint8)), (T.lsn[:, 160:384], T.fs[:])])
-            send(asker, owner, "a_f2", "fq", "lF2", 143000, [(T.lq[:, 216:384].bitcast(dt.uint8), T.fq[:, 56:224].bitcast(dt.uint8))])
-            dma("y", "ld_v", "lF0", "vt", T.vt[:], T.v[:], 131072)
-            quant("vt", "vq", T.vq[:], T.vs[:], T.vt[:], 128)
+        xt, ca, a, hs, ax = "xt%d" % t, "ca%d" % t, SPLIT[t], DC + K * t, AX[t]
+        x0 = float(SH - hs)
+        move(jd[t], IND(INV(0), W("tgu")) if t == 0 else IND(W("jw%d" % t), B("tpu", t - 1)))
+        scan(B("jl", t), W("sel16"), jd[t], 0.0, OP.mult, OP.add)
+        lin(B("xx", t), B("jl", t, 15, P, 16), pc(8), x0)
+        tt(DS(t, 1), B("xx", t), W("pd"), OP.min)
+        nm = W("ca1", A) if t == 1 else B("nm", t, 0, A)
         if t == 1:
-            move("ir12 job1", "jw2c", T.jw2[:, P + K:P + 2 * K], T.ir12[:].indirect(jk), K)
-            send(owner, asker, "a_l1", "ls1", "lr1", 2048, [(T.lr1[:], B("ls", 1, 0, 8))])
-            move("mt lr1", "F1", T.ft[:, 0:128], T.mt[:].indirect(T.lr1[:]), 128)
-            quant("F1 F0 F20 F21 F22 F23", "f1q", T.f1q[:], T.f1s[:], T.ft[:, 0:512], 128)
-            send(asker, owner, "a_f1", "f1q", "", 16384, [(T.lq[:, 0:K].bitcast(dt.uint8), T.f1q[:, 0:K].bitcast(dt.uint8))])
-            send(asker, owner, "a_f1", "f1q", "lF1", 20480, [(T.lsn[:, 0:K], T.f1s[:, 0:K])], before=1)
-        marks(t)
-        tt("c16", k("m2# ps%d" % MARKS), B("m2", t), pm, T.c16[:], OP.max, P)
-        tt(k("hm#"), k("kk# ps%d" % MARKS), B("kk", t), pm, B("hm", t), OP.add, P)
-        scan(k("m2# r16"), k("pv#"), B("pv", t), T.r16[:], B("m2", t), 0.0, OP.max, OP.min, P)
-        unpack(t)
-        if t < 2:
-            tt(k("acc# c2#"), k("s3#"), B("s3", t), acc[t], B("c2", t), OP.max, 2 * A)
+            tt(nm, IND(W("jd1"), W("pl")), W("yrow", K, K + A), OP.not_equal)
         else:
-            lin("c22", "s1", T.s1[:], B("c2", t), 400.0, 13000.0, A)
-            tt("s1 jrow", "s2", T.s2[:], T.s1[:], T.jrow[:], OP.min, 2 * A)
-            tt("acc2 s2", "s32", B("s3", t), acc[t], T.s2[:], OP.max, 2 * A)
-        tt(k("s3# mask4"), k("s4#"), B("s4", t), B("s3", t), T.mask4[:], OP.mult, 2 * A)
-        scan(k("s4# keep4"), k("s5#"), B("s5", t), T.keep4[:], B("s4", t), 0.0, OP.mult, OP.add, 96)
-        c = 4 if t < 2 else 5
-        ts(k("s5# zc0 zc2"), k("zo#"), B("zo", t), B("s5", t, 3, A, 4), 4.0, OP.mult, T.pc[:, c:c + 1], OP.add)
+            if t == 2:
+                ts(W("oj"), DS(t, 1), SH + 0.25, OP.add)
+                cp(IND(W("ca2", A), W("oj")), places)
+            ts(nm, W(ca, ax, ax + A), K + 8.0, OP.is_gt)
+        scan(W(ca, 0, ax), W(nm[0], nm[1], nm[1] + ax), W("cap", 0, ax), float(K), OP.add, OP.min)
+        for i in range(2):
+            act(B("sj", t, ax * i, ax * i + ax - 1), W(ca, 0, ax - 1), AF.Sign, -1.0, pc(6 + i), B("js", t, i, i + 1))
+        ts(B("jo", t), B("js", t), 0.5, OP.mult, (ax - 1) / 2 + 0.25, OP.add)
+        s = P + K * t
+        move(W("tw", s, s + K), IND(W("iot", AW[t], AW[t] + ax), B("jo", t)))
+        move(W("tw", s + K, s + 2 * K), IND(W("iot", 0, ax), B("jo", t)))
+        scan(B("gs", t), W("sel4", 0, 64), W("tw", s, s + 2 * K), 0.0, OP.mult, OP.add)
+        ts(B("lst", t), B("gs", t, 3, 64, 4), sc4, OP.mult, pc(5), OP.add)
+        if t < 2:
+            send(owner, asker, "a_l%d" % t, [(W("lr", 8 * t, 8 * t + 8), B("lst", t, 0, 8))])
+            scan(B("al", t), W("sel16", 0, K), W("tw", s, s + K), 0.0, OP.mult, OP.add)
+            ts(B("alu", t), B("al", t, 15, K, 16), pc(9), OP.mult, 0.25, OP.add)
+            for i in range(t + 1, R):
+                move(W("jw%d" % i, s, s + K), IND(INV(i, K), B("alu", t)))
+            f0, q0, lq, ls = [(512, 96, 0, 0), (0, 0, 160, 256)][t]
+            move(W("ft", f0, f0 + 128), IND(W("mt"), W("lr", 8 * t, 8 * t + 8)))
+            quant(W("fq", 128 * t, 128 * t + 128), W("fs", 128 * t, 128 * t + 128), W("ft", f0 - 4 * q0, f0 - 4 * q0 + 512))
+            send(asker, owner, "a_f%d" % t, [(bytes_of("lq", lq, lq + K), bytes_of("fq", 128 * t + q0, 128 * t + q0 + K)),
+                                             (W("lsn", ls, ls + 128), W("fs", 128 * t, 128 * t + 128))])
+        if t == 0:
+            move(W("jd1", 0, K), IND(INV(1, K), B("alu", 0)))
+            cp(IND(W("at0"), B("alu", 0)), W("prow", 0, K))
+            move(W("v1"), IND(W("at0"), adu[1]))
+            scan(W("v16"), W("sel16", 0, A), W("v1"), 0.0, OP.mult, OP.add)
+            ts(W("pl"), W("v16", 15, A, 16), pc(9), OP.mult, P - 1 + 0.25, OP.add)
+            scan(W("v4"), W("sel4", 0, A), W("v1"), 0.0, OP.mult, OP.add)
+            ts(W("v4m"), W("v4", 3, A, 4), pc(13), OP.min)
+        marks(t)
+        tt(B("m2", t), pm, W("c16"), OP.add)
+        tt(B("kk", t), pm, jd[t], OP.add)
+        scan(B("pv", t), W("r16"), B("m2", t), 0.0, OP.max, OP.min)
+        vq, vs, cols, o, w = [(0, 96, 128, 0, K), (64, 160, 128, 96, K), (192, 384, A, 0, A)][t]
+        for b in range(4):
+            mm(4 + b, W("eq", 128 * b, 128 * b + 128), W("es", 128 * b, 128 * b + 128), W("lq", vq, vq + cols), W("lsn", vs, vs + cols))
+            move(W(xt, 4 * DC + b, 4 * (DC + w), 4), bank(4 + b, o, w))
+        scan(B("zl", t, 0, ax + A), W("sel4", 0, ax + A), W(ca, 0, ax + A), 0.0, OP.mult, OP.add)
+        cl, al = B("zl", t, 3, A, 4), B("zl", t, ax + 3, ax + A, 4)
+        zm = [B("zm", t, 48 * i, 48 * i + 48) for i in range(3)]
+        if t == 0:
+            tt(zm[0], cl, al, OP.min)
+        elif t == 1:
+            ts(zm[2], al, 1000.0, OP.mult, pc(14), OP.add)
+            tt(zm[1], zm[2], cl, OP.min)
+            tt(zm[0], zm[1], W("v4m"), OP.max)
+        else:
+            ts(zm[2], cl, pc(15), OP.subtract, 1000.0, OP.mult)
+            tt(zm[1], zm[2], W("j4"), OP.max)
+            tt(zm[0], zm[1], al, OP.min)
+        ts(B("zo", t), zm[0], sc4, OP.mult, pc(10 if t == 1 else 4), OP.add)
         for h in range(2):
-            move(k("zo# D# D#z D#0 D#1 D#2 D#3 X# X#0 X#1 X#2 X#3"), k("zz#%d" % h), B("zz", t, 384 * h, 384 * h + 384),
-                 xt[t][:, 0:xbase[t] + 4 * P].indirect(B("zo", t, 24 * h, 24 * h + 24)), 384)
-        quant(k("zz#0 zz#1"), "zq", T.zq[:], T.zs[:], B("zz", t), A)
-        e = xbase[t] + 4 * P
+            move(B("zz", t, 384 * h, 384 * h + 384), IND(W(xt, 4 * (XC - K if t == 1 else XC), 4 * ZC[t] + 16), B("zo", t, 24 * h, 24 * h + 24)))
+        quant(W("zq"), W("zs"), B("zz", t))
         for b in range(4):
-            mm("zq wq wsn", b, T.wq[:, 128 * b:128 * b + 128], T.wsn[:, 128 * b:128 * b + 128], T.zq[:], T.zs[:], A)
+            mm(b, W("wq", 128 * b, 128 * b + 128), W("wsn", 128 * b, 128 * b + 128), W("zq"), W("zs"))
         for b in range(4):
-            out, src = xt[t][:, e + b:e + 4 * A:4], T.ps[:, 512 * b:512 * b + A]
-            node("", k("ps%d H#%d" % (b, b)), {"s": (lambda q, out=out, src=src: q.activation(out, src, AF.Relu, scale=0.03125), "e", A),
-                                               "v": (lambda q, out=out, src=src: q.tensor_scalar(out, src, 0.0, 0.03125, OP.max, OP.mult), "e", A)})
-        move(k("H#0 H#1 H#2 H#3 ls#"), k("HS#"), xt[t][:, e + 4 * A:e + 4 * A + 4 * K], xt[t][:, e:e + 4 * A].indirect(B("ls", t, 8, 16)), 128)
+            out, src = W(xt, b, 4 * A, 4), bank(b, 0, A)
+            node([src], [out], {"s": lambda q, out=out, src=src: q.activation(ap(out), ap(src), AF.Relu, scale=0.03125),
+                                "v": lambda q, out=out, src=src: q.tensor_scalar(ap(out), ap(src), 0.0, 0.03125, OP.max, OP.mult)})
+        move(W(xt, 4 * hs, 4 * hs + 4 * K), IND(W(xt, 0, 4 * ax), B("lst", t, 8, 16)))
+        if t == 0:
+            move(W("xt1", 4 * (XC - K), 4 * XC), IND(W(xt, 0, 4 * ax), B("lst", t, 8, 16)))
         for c in range(16):
             h, piv, o = 16 * c + 16, B("pv", t, 16 * c + 15, 16 * c + 16), P * c
-            lo, hi = T.cmp[:, o:o + h], T.cmp[:, o + h:o + P]
-            if c < a:
-                act(k("kk# pv#"), "cma%d cmb%d" % (c, c), T.cmp[:, o:o + P], B("kk", t), AF.Sign, P, scale=-1.0, bias=piv)
-                act("", k("cma%d gb#_%d" % (c, c)), lo, lo, AF.Relu, max(64, h) + 20, scale=-1.0, accum_out=B("gb", t, c, c + 1))
-                act("", k("cmb%d ra#_%d" % (c, c)), hi, hi, AF.Relu, max(64, P - h) + 20, accum_out=B("ra", t, c, c + 1))
-            else:
-                ts(k("kk# pv#"), "cma%d" % c, lo, B("kk", t, 0, h), piv, OP.is_le, c=h)
+            lo, hi = W("cmp", o, o + h), W("cmp", o + h, o + P)
+            if c >= a:
+                act(W("cmp", o, o + P), B("kk", t), AF.Sign, -1.0, piv)
+                act(lo, lo, AF.Relu, -1.0, 0.0, B("gb", t, c, c + 1))
                 if h < P:
-                    ts(k("kk# pv#"), "cmb%d" % c, hi, B("kk", t, h, P), piv, OP.is_lt, c=P - h)
-                scan("cma%d cmb%d" % (c, c), "cnt%d" % c, T.cnt[:, 128 * c:128 * c + 128], T.cmp[:, o:o + 128], T.cmp[:, o + 128:o + P], 0.0, OP.add, OP.add, 64)
-        tt(k("pv# kk#"), k("eqd#"), B("eqd", t), B("pv", t), B("kk", t), OP.is_equal, 2 * P)
-        scan(k("eqd# keep16"), k("cor#"), B("cor", t), T.keep16[:], B("eqd", t), 0.0, OP.mult, OP.add, 128)
-        act(k("jd#"), k("d0#"), D(0), JD, AF.Relu, scale=4000.0, bias=-192.5 * 4000.0)
-        act(k("jd#"), k("d1#"), D(1), JD, AF.Relu, scale=-2000.0, bias=192.5 * 2000.0)
-        ts(k("c2#"), k("th#"), B("th", t, 0, 1), B("c2", t, A - 1, A), -32.0, OP.max, HZ + 0.5, OP.add)
-        tt(k("jd# d0#"), k("d2#"), D(2), JD, D(0), OP.subtract)
-        o = 16 * SPLIT.index(a)
-        tt(k("d1# cbs%d cbv%d" % (a, a)), k("d3#"), D(3), T.cb[:, o:o + 16], D(1), OP.subtract)
-        tt(k("d2# pdm"), k("d4#"), D(4), D(2), T.pdm[:], OP.max)
-        tt(k("d3# cor#"), k("d5#"), D(5), D(3), B("cor", t, 15, P, 16), OP.add)
-        tt(k(" ".join("gb#_%d ra#_%d" % (c, c) for c in range(a))), k("d6#"), D(6, 0, a), B("gb", t, 0, a), B("ra", t, 0, a), OP.subtract)
-        tt(k("d5# d6#"), k("d7a#"), D(7, 0, a), D(5, 0, a), D(6, 0, a), OP.add)
-        tt(k("d5# ") + " ".join("cnt%d" % c for c in range(a, 16)), k("d7b#"), D(7, a), D(5, a), T.cnt[:, 128 * a + 127:2048:128], OP.subtract)
-        ts(k("d7a# d7b# th#"), k("d8#"), D(8), D(7), B("th", t, 0, 1), OP.subtract, 4096.0, OP.mult)
-        tt(k("d7a# d7b# d8#"), k("d9#"), D(9), D(7), D(8), OP.min)
-        tt(k("d9# d4#"), k("d10#"), D(10), D(9), D(4), OP.max)
-        lin(k("d9#"), k("d11#"), D(11), D(9), 1.0, float(P + K - 1 - HZ + K * t))
-        tt(k("d11# pd tpf%d" % (t - 1)), k("tpf#"), B("tpf", t), D(11), T.pd[:] if t == 0 else B("tpf", t - 1), OP.max)
-        cp(k("tpf#"), k("tpu#"), B("tpu", t), B("tpf", t))
+                    act(hi, hi, AF.Relu, 1.0, 0.0, B("ra", t, c, c + 1))
+            else:
+                ts(lo, B("kk", t, 0, h), piv, OP.is_le)
+                if h < P:
+                    ts(hi, B("kk", t, h, P), piv, OP.is_lt)
+                scan(W("cnt", 128 * c, 128 * c + 128), W("cmp", o, o + 128), W("cmp", o + 128, o + P), 0.0, OP.add, OP.add)
+        tt(B("eqd", t), B("pv", t), B("kk", t), OP.is_equal)
+        scan(B("cor", t), k16[t], B("eqd", t), 0.0, OP.min, OP.add)
+        ts(B("th", t, 0, 1), W(ca, A - 1, A), 2.0 * K, OP.min, -x0 - K - 0.5, OP.add)
+        tt(B("e1", t), B("cor", t, 15, P, 16), B("xx", t), OP.add)
+        tt(DS(t, 0, 0, a), W("cnt", 127, 128 * a, 128), B("e1", t, 0, a), OP.subtract)
+        if a < 16:
+            tt(B("e2", t, a, 16), B("gb", t, a, 16), B("e1", t, a, 16), OP.add)
+            tt(DS(t, 0, a), B("ra", t, a, 16), B("e2", t, a, 16), OP.subtract)
+        ts(W("d0", 1, 48, 3), DS(t), B("th", t, 0, 1), OP.subtract, -4096.0, OP.mult)
+        scan(W("ds", 48 * t + 48, 48 * t + 96), W("d0"), W("ds", 48 * t, 48 * t + 48), 0.0, OP.min, OP.max)
+        ts(B("tpu", t), DS(t + 1, 2), SH - XC + 0.25, OP.add)
+        nx = X(t + 1)
         for e in range(4):
-            ts(k("d10#"), k("xo#%d" % e), B("xo", t, 16 * e, 16 * e + 16), D(10), 4.0, OP.mult, 4.0 * (P - 1) + e, OP.add)
-            move(k("X# X#0 X#1 X#2 X#3 H#0 H#1 H#2 H#3 HS# xo#%d" % e), "X%d%d" % (t + 1, e), xt[t + 1][:, xbase[t + 1] + e:xbase[t + 1] + 4 * P:4],
-                 xt[t][:, xbase[t]:xbase[t] + 4 * XW].indirect(B("xo", t, 16 * e, 16 * e + 16)), P)
+            ts(B("xo", t, 16 * e, 16 * e + 16), DS(t + 1, 1), 4.0, OP.mult, 4.0 * SH + e + 0.25, OP.add)
+            move(W(nx[0], nx[1] + e, nx[2], 4), IND(W(xt, 0, 4 * hs + 4 * K), B("xo", t, 16 * e, 16 * e + 16)))
 
     for t in range(R):
         one_round(t)
 
-    marks(3)
-    move("twa tw0 tw1 tw2 tpu2", "otb", T.otb[:], T.tw[:].indirect(B("tpu", 2)), P)
-    dma("y", "st1", "xq", "", T.oc[:], T.xq[:].bitcast(dt.uint8), 131072)
+    marks(R)
+    move(W("otb"), IND(W("tw", 0, P + R * K), B("tpu", R - 1)))
+    dma("st", [W("otb")], [], T.ot[:], T.otb[0:128:16, :])
+    dma("st", [W("xq")], [], T.oc[:], ap(RAW(W("xq"), dt.uint8)))
     for i in range(4):
-        dma("g" if i > 1 else "y", "st3" if i > 1 else "st1", "xq", "", T.osc[4 * i:4 * i + 4, :], T.xs[32 * i:32 * i + 4, :], 1024)
-    move("", "yb ps%d" % MARKS, T.yb[:], pm, P, "e")
-    dma("s", "st2", "otb", "", T.ot[:], T.otb[0:128:16, :], 8192)
-    dma("s", "st2", "yb", "", T.y[:], T.yb[:], 131072)
+        dma("st", [W("xs")], [], T.osc[4 * i:4 * i + 4, :], T.xs[32 * i:32 * i + 4, :])
+    move(W("yb"), pm)
+    dma("st", [W("yb")], [], T.y[:], T.yb[:])
     return nodes
 
 
 def rank_program(g, core, T, topo):
     if T.rank_of(core) is None:
         return
-    nodes = calls(g, core, T, topo)
+    nodes = calls(core, T, topo)
+    plan = [(int(w[:-1]), w[-1]) for w in ORDER.split()] or [(i, list(nd["alts"])[0]) for i, nd in enumerate(nodes)]
     queue = {"v": g.vector, "s": g.scalar, "p": g.tensor, "g": g, "y": g.sync}
-    total, seen, event = {}, {}, {}
+    total, event, known = {}, {}, {q: {} for q in queue}
 
-    def need(q, s, v):
-        if seen.get((q, s), 0) < v:
-            queue[q].wait_ge(T.sem[s], v)
-            seen[(q, s)] = v
+    def need(q, events):
+        for s, v, before in events:
+            if known[q].get(s, 0) < v and not any(b.get(s, 0) >= v or (s2 == s and v2 > v) for s2, v2, b in events):
+                queue[q].wait_ge(T.sem[s], v)
+        for s, v, before in events:
+            for s2, v2 in list(before.items()) + [(s, v)]:
+                known[q][s2] = max(known[q].get(s2, 0), v2)
 
-    for i, q in PLAN:
+    for i, q in plan:
         nd = nodes[i]
         if nd["arrival"]:
-            event[i] = nd["arrival"]
+            event[i] = nd["arrival"] + ({},)
             total[event[i][0]] = event[i][1]
             continue
-        want = {}
-        for j in nd["deps"]:
-            if event[j]:
-                want[event[j][0]] = max(want.get(event[j][0], 0), event[j][1])
-        for s in sorted(want):
-            need(q, s, want[s])
-        ins = nd["alts"][q][0](queue[q])
+        need(q, [event[j] for j in nd["deps"]])
+        ins = nd["alts"][q](queue[q])
         s = nd["sem"] or "c" + q
         total[s] = total.get(s, 0) + nd["inc"]
-        if s == "sent":
-            event[i] = None
-        else:
+        if s != "sent":
             ins.then_inc(T.sem[s], nd["inc"])
-            event[i] = (s, total[s])
+            event[i] = (s, total[s], dict(known[q]))
     for s in sorted(total):
-        need("g", s, total[s])
+        need("g", [(s, total[s], {})])

@@ -10,28 +10,29 @@ AW = [MC + K, MC + 2 * K + A, MC + 2 * K + 2 * A]
 PV = P - 1 - K
 SH = 1024
 UNIT, LIFT = 2.0 ** 70, 2.0 ** 30
-SPLIT = [10, 10, 10]
+SPLIT = [8, 11, 10]
 ORDER = """
-0y 8g 19v 1y 3s 2y 15v 7y 4s 9g 36s 5y 56v 16v 13g 37v 55v 23v 21v 11g 64v 22v 20v 71v 24v 61v 75v 33s 25s 30s 29s 72v
-76s 10g 31v 46v 86v 45v 47v 70v 77s 12g 107v 38v 57g 42s 52s 108v 110s 109s 39v 88v 17g 133v 40v 35s 87s 111v 78v 113s 134p 28s 112s 114v
-26s 53s 32s 135v 103s 115v 41v 116g 136v 137v 192s 80v 85s 174v 186v 204s 162v 165v 184v 194s 171v 169v 172v 34s 73g 195s 178v 43s 63g 175v 201s 117x
-58v 207s 104v 18g 197s 118v 74x 198s 211v 163v 196s 209v 105s 202s 193s 119v 168v 166v 122s 187v 177v 44s 190v 200s 208s 123v 124g 125x 183v 203s 82v 205s
-79s 60g 65g 199s 210v 106v 126s 167v 189v 6s 83s 180v 173v 188v 181v 179v 121s 191v 176v 120s 212v 182v 14g 206s 170v 185v 214v 164v 62g 127v 213v 215v
-94v 128s 67v 140p 216v 69v 84s 217v 66v 218v 129v 146v 227s 130v 68v 144p 142p 92v 225v 48v 231v 49s 147v 138p 232v 143s 148v 145s 141s 139v 233s 219v
-223v 150v 149s 151v 234s 235v 262v 152p 236s 237v 90v 154p 238v 328v 156s 50v 155p 239v 240g 242v 158s 263v 131v 89v 96v 264v 159v 153p 157s 228v 132v 93s
-160v 241x 95s 243v 221v 224v 226s 220v 222s 244s 249v 245s 265v 91s 27v 250p 246v 247g 229v 230v 161s 266v 97s 251v 252v 81s 253v 98v 321s 326v 300v 101g
-102x 324s 309s 298v 315s 289v 307v 327v 59g 310s 304v 248x 258p 51s 318s 295v 291v 306v 312s 279v 54v 283v 320s 325s 329v 294v 316s 282v 297v 280v 323s 322s
-288v 292v 319s 260p 286v 314s 313s 293v 256p 308v 301v 259s 254p 261s 284v 303v 257s 285v 311s 296v 331v 255s 290v 317s 302v 287v 268s 299v 305v 281v 332v 330v
-333v 267s 334v 335v 336v 340v 344s 269v 271p 345v 272p 342v 338v 275s 346v 347v 270p 276s 348v 349v 273p 274s 350v 351v 277s 99g 100x 368p 278s 366p 343s 370p
-337v 364p 339s 372v 373v 341s 371s 352s 359v 360p 367s 374v 365v 353s 375v 376v 369s 354v 361v 378s 362v 363v 356v 355s 377s 395v 407v 408v 389v 392v 436v 422s
-434s 379v 396v 409v 431s 390v 428s 413v 437v 404v 425s 429s 424s 393v 399v 419s 426s 433s 410v 402v 423s 401v 391v 411v 421s 427s 382p 383p 435s 381p 417v 414v
-416v 397v 432s 412v 405v 420s 403v 394v 398v 418v 439v 415v 430s 400v 385s 406v 441v 386s 438v 440v 380p 384s 442v 357v 387s 443v 358v 444v 388s 452v 453s 446v
-448v 449s 450v 447v 451v 454v 460s 455p 445v 459y 462s 461y 456v 458y 463s 464y 457y
+8g 0s 16v 3y 1y 2s 4y 9g 6y 23v 24v 22v 17v 10g 11s 13s 25v 20v 21g 38v 34s 61v 31s 12g 30s 39s 44s 76v 32v 46v 80v 50s
+14s 45g 33s 57s 26s 37s 49s 47s 48s 40s 77v 91v 29s 78g 112s 83v 92s 81s 113v 138v 115s 93v 114s 51v 151v 108s 139p 15g 52v 116v 42v 69g
+41v 82s 140v 79x 141v 118s 117s 142v 36s 119v 182v 203s 120v 180v 200s 121g 177v 215s 214v 63g 191s 66g 206s 62g 188v 197s 122x 43v 18g 209s 198s 183v
+192s 168v 207s 179v 167v 202s 216v 204s 184v 170v 171v 123v 127s 109v 205s 194s 128v 189v 27s 129g 185v 193s 174v 110s 199s 70g 172v 201s 173v 218v 176v 211s
+124v 212s 190v 85v 195s 210s 35s 196s 208s 60g 213s 186v 169v 175v 125s 178v 181v 187v 217v 131s 220v 5s 130x 88s 152v 111v 219v 221v 132v 65g 72v 133s
+222v 67g 153v 71v 19g 223v 75v 84s 224v 74v 231v 134v 73v 233s 229v 143p 135v 53v 145p 99v 149p 146s 144s 237v 147p 150s 148s 97v 154s 64g 238v 155v
+239s 234v 240s 156v 241v 160p 243s 242v 100s 159p 244v 225v 245v 158p 268v 163s 246g 227v 157p 95v 28s 164s 162v 55s 101v 87v 161s 165s 247x 333s 269s 166y
+232s 230v 228s 226v 251s 255v 54s 86s 252v 256p 126v 253g 136v 248v 98s 137v 68g 270v 257v 102s 258v 96s 271v 259v 89s 103v 289v 106g 288v 321s 272v 316v
+104g 313v 318s 254x 294v 306v 335v 322s 286v 330s 292v 319s 300v 301v 235s 304v 58s 327s 295v 107x 331s 332v 260p 7s 264p 309v 261s 324s 266p 285v 297v 290v
+262p 56v 265s 334v 267s 291v 263s 298v 329s 274s 296v 310v 336v 236v 315v 249v 303v 312v 273s 305v 287v 307v 105x 320s 328s 275v 317v 325s 308v 277p 299v 314v
+302v 444s 311v 326s 276p 338v 323s 293v 339v 278p 337v 280s 94v 340v 279p 250v 282s 341v 281v 371p 283s 342v 343v 349v 373p 351s 345v 284v 375p 347v 350v 346s
+348v 344s 352v 366v 353s 374s 372v 367p 90s 354v 355v 377p 368v 59s 376s 369v 378s 370v 356v 426s 438s 432s 440s 427s 439s 396v 418v 357v 441s 417v 358v 429s
+400v 360s 379v 397v 380s 435s 406v 381v 359s 398v 421v 433s 382v 408v 436s 415v 383v 361v 431s 403v 384s 399v 443v 420v 385s 423v 401v 445v 402v 424v 414v 419v
+442s 404v 386v 430s 405v 447v 388p 411v 437s 409v 428s 434s 387p 407v 363s 412v 362s 449v 390p 410v 392s 425v 416v 413v 391s 389p 422v 364v 450v 394s 446v 448v
+365v 393s 451v 452v 395s 460v 454v 463v 457v 462v 456s 465v 459s 458v 461s 473v 464s 455v 474p 477y 453v 468v 475s 466s 469p 472y 478y 481y 479y 476y 480y 470v
+471s 467y
 """
 PER_ROUND = {"jl": (P, F32), "xx": (16, F32), "nm": (A + K, BF), "sj": (2 * (A + K), BF), "js": (2, F32),
              "jo": (2, U16), "gs": (64, F32), "lst": (16, U16), "al": (K, F32), "alu": (2, U16), "zl": (2 * A + K, BF), "zm": (4 * 48, F32), "zo": (48, U16),
              "zz": (4 * A, BF), "m2": (P, F32), "pv": (P, F32), "kk": (P, F32), "eqd": (P, BF), "cor": (P, BF), "ra": (16, F32), "gb": (16, F32),
-             "e1": (16, F32), "e2": (16, F32), "th": (2, F32), "tpu": (16, U16), "xo": (64, U16), "k16": (P, BF)}
+             "e1": (16, F32), "e2": (16, F32), "th": (2, F32), "tpu": (16, U16), "xo": (64, U16)}
 WIDTH = {
     "tg32": (16, I32), "ad32": (36, I32), "tgu": (16, U16), "adu": (36, U16), "lr": (16, U16), "l2r": (16, U16), "l2o": (48, U16),
     "mt": (4 * (MC + K), BF), "ft": (640, BF), "ft2": (4 * A, BF), "fq": (256 + A, CODE), "fs": (256 + A, U8),
@@ -41,10 +42,10 @@ WIDTH = {
     "vq": (128, CODE), "vs": (128, U8), "uoff": (8, U16), "wq": (512, CODE), "wsn": (512, U8),
     "xt0": (4 * (ZC[0] + 4), BF), "xt1": (4 * (ZC[1] + K), BF), "xt2": (4 * (ZC[2] + 4), BF), "xt3": (4 * P, BF),
     "xq": (P, CODE), "xs": (P, U8), "zq": (A, CODE), "zs": (A, U8),
-    "iot": (AW[2] + A, F32), "inv": (R * MC + K, F32), "at0": (MC + K, BF), "cap": (A + K, BF), "prow": (K + P, BF), "yrow": (P, F32),
+    "iot": (AW[2] + A, F32), "inv": (R * (MC + K), F32), "at0": (MC + K, BF), "cap": (A + K, BF), "prow": (K + P, BF), "yrow": (P, F32),
     "ca0": (2 * A + K, BF), "ca1": (2 * A, BF), "ca2": (A + DC, BF), "oj": (16, U16),
     "jd0": (P, F32), "jd1": (P + 2 * K + 8, F32), "jd2": (P, F32), "v1": (A, BF), "v16": (A, BF), "v4": (A, BF), "v4m": (48, F32), "pl": (12, U16), "j4": (48, F32),
-    "pat16": (P, BF), "pat4": (2 * A + K, BF), "sa": (P, BF), "sb": (P, BF), "sel16": (P, BF), "sel4": (2 * A + K, BF), "c16": (P, BF), "r16": (P, BF),
+    "pat16": (P, BF), "sa": (P, BF), "sb": (P, BF), "sel16": (P, BF), "sel4": (2 * A + K, BF), "c16": (P, BF), "r16": (P, BF), "k16": (P, BF),
     "pi": (4, I32), "pj": (4, I32), "pc": (24, F32), "t4": (16, F32), "pd": (16, F32), "ds": (48 * (R + 1), F32), "d0": (48, F32),
     "jw1": (P + K, F32), "jw2": (P + 2 * K, F32), "tw": (P + 4 * K, F32), "cmp": (16 * P, BF), "cnt": (16 * 128, BF),
     "yb": (P, F32), "otb": (P, F32), "ps": (4096, F32),
@@ -53,7 +54,7 @@ for _n in PER_ROUND:
     WIDTH[_n] = (R * PER_ROUND[_n][0], PER_ROUND[_n][1])
 SCRATCH = {_n: ("psum" if _n == "ps" else "sbuf", [128, WIDTH[_n][0]], WIDTH[_n][1]) for _n in WIDTH}
 LOADS = ["tg", "ad", "x", "u", "m", "wc", "ws", "v"]
-SEMAPHORES = ["cv", "cs", "cp", "cg", "sent", "st", "a_l0", "a_l1", "a_l2", "a_f0", "a_f1", "a_f2", "a_s2"] + ["ld_" + n for n in LOADS]
+SEMAPHORES = ["cv", "cs", "cp", "cg", "sent", "st", "a_l0", "a_l1", "a_l2", "a_f0", "a_f1", "a_f2", "a_s2", "c_jd", "c_hs"] + ["ld_" + n for n in LOADS]
 
 
 def W(name, a=0, b=None, step=1):
@@ -76,7 +77,7 @@ def RAW(view, d):
 def calls(core, T, topo):
     rank, n = T.rank_of(core), len(T.cores)
     owner, asker = T.cores[(rank + 1) % n], T.cores[(rank - 1) % n]
-    nodes, touched = [], {}
+    nodes, touched, sends = [], {}, []
 
     def ap(x):
         if not isinstance(x, tuple):
@@ -125,7 +126,8 @@ def calls(core, T, topo):
             h = len(es) // 2
             return e.remote_dma_fused([RemoteDMATransfer(dst_ids=[DstId(rid=rid, pnc=pid)], dma_engine_mask=bits(es[h * i:h * i + h]), remote_sem=T.sem[sem],
                                                          src=ap(pairs[i][1]), dst=ap(pairs[i][0])) for i in range(2)], local_sem=T.sem.sent)
-        i = node([p[1] for p in pairs], [], {"g": f}, "send " + sem, sem="sent", inc=len(es))
+        i = node([p[1] for p in pairs], [], {"g": f}, "send " + sem, sem="sent", inc=len(es), after=sends[:1])
+        sends.append(i)
         node([], [p[0] for p in pairs], {"x": None}, sem, arrival=(sem, len(lanes(src, core))), after=[i])
 
     def ts(out, a, s1, o1, s2=None, o2=None):
@@ -178,6 +180,14 @@ def calls(core, T, topo):
     def load(name, view):
         dma("ld_" + name, [], [view], ap(view), T[name][:])
 
+    def copy(sem, out, a):
+        dma(sem, [a], [out], ap(out), ap(a))
+
+    def ramp(out, width, base, src):
+        node([src], [out], {"g": lambda e: e.iota(ap(out), [[1, width]], base, 0, allow_small_or_imprecise_dtypes=True),
+                            "s": lambda e: e.activation(ap(out), ap(src), AF.Identity, bias=float(base + P - 1)),
+                            "v": lambda e: e.tensor_scalar(ap(out), ap(src), float(base + P - 1), None, OP.add)})
+
     def pc(i):
         return W("pc", i, i + 1)
 
@@ -188,7 +198,7 @@ def calls(core, T, topo):
         return W("ds", 48 * t + 3 * a + e, 48 * t + 3 * b, 3)
 
     def INV(t, more=0):
-        return W("inv", MC * t, MC * t + MC + more)
+        return W("inv", (MC + K) * t, (MC + K) * t + MC + more)
 
     def bytes_of(name, a, b):
         return RAW(W(name, a, b), dt.uint8)
@@ -210,13 +220,14 @@ def calls(core, T, topo):
     node([], [W("pi", 0, 1)], {"g": lambda e: e.iota(ap(W("pi", 0, 1)), [[0, 1]], 0, 1)})
     steps(W("prow"), [[1, K + P]], 1 - P)
     steps(W("pat16"), [[0, 16], [1, 16]], 0)
-    steps(W("iot", 0, MC + K), [[1, MC + K]], 0)
-    steps(W("iot", AW[0] + A, AW[1]), [[1, K]], MC)
-    steps(W("pat4"), [[0, (2 * A + K) // 4], [1, 4]], 0)
+    for a in range(0, MC + K, K + P):
+        w = min(K + P, MC + K - a)
+        ramp(W("iot", a, a + w), w, a, W("prow", 0, w))
+    ramp(W("iot", AW[0] + A, AW[1]), K, MC, W("prow", 0, K))
     steps(W("d0"), [[0, 16], [30000, 3]], -30000)
     fill(W("at0"), 2 * K + 1)
     fill(INV(0), 0)
-    fill(INV(1), 0)
+    fill(INV(1, K), 0)
     fill(INV(2, K), 0)
     fill(W("cap"), 2 * K + 1)
     fill(B("nm", 0, A), 1)
@@ -237,30 +248,27 @@ def calls(core, T, topo):
     lin(DS(0, 2), W("prow", K, K + P, 16), 1.0, pc(11))
     lin(W("yrow"), places, -UNIT, (2 * SH - DC - PV) * UNIT)
     ts(W("uoff"), W("prow", K, K + 128, 16), float(PV), OP.add)
-    ts(W("c16"), W("pat16"), pc(0), OP.not_equal, 2.0 ** 90, OP.mult)
+    lin(pc(17), pc(0), -2.0 ** 90, 0.0)
+    node([W("pat16"), pc(0), pc(17)], [W("c16")], {"v": lambda e: e.tensor_scalar(ap(W("c16")), ap(W("pat16")), ap(pc(0)), 2.0 ** 90, OP.not_equal, OP.mult),
+                                                   "s": lambda e: e.activation(ap(W("c16")), ap(W("pat16")), AF.Abs, scale=2.0 ** 90, bias=ap(pc(17)))})
     ts(W("sa"), W("pat16"), pc(0), OP.not_equal)
     ts(W("sb"), W("pat16"), pc(3), OP.is_equal, LIFT, OP.mult)
     tt(W("sel16"), W("sa"), W("sb"), OP.max)
     lin(W("r16"), W("pat16"), -2.0 ** 96, 2.0 ** 95)
-    k16 = []
-    for t in range(R):
-        a, o = SPLIT[t], SPLIT.index(SPLIT[t])
-        k16.append(B("k16", o))
-        if o == t:
-            lin(B("k16", t), W("pat16"), 512.0, 0.0)
-            if a < 16:
-                lin(B("k16", t, 16 * a, P, 16), W("prow", K + 16 * a, K + P, 16), -1.0, float(-PV - 16))
-    ts(W("sel4"), W("pat4"), pc(2), OP.is_gt, 2.0 ** 20, OP.mult)
-    ts(W("t4", 0, 4), W("pat4", 0, 4), pc(2), OP.is_le, 2.0 ** -10, OP.max)
+    steps(W("k16"), [[0, 16], [512, 16]], 0)
+    ts(W("t4", 8, 12), W("pat16", 0, 4), pc(2), OP.is_gt, 2.0 ** 20, OP.mult)
+    for e in range(4):
+        lin(W("sel4", e, 2 * A + K, 4), W("prow", 0, (2 * A + K) // 4), 0.0, W("t4", 8 + e, 9 + e))
+    ts(W("t4", 0, 4), W("pat16", 0, 4), pc(2), OP.is_le, 2.0 ** -10, OP.max)
     scan(W("t4", 4, 8), W("t4", 0, 4), W("t4", 0, 4), 4.0, OP.mult, OP.mult)
     sc4 = W("t4", 7, 8)
     node([sc4], [pc(12)], {"v": lambda e: e.reciprocal(ap(pc(12)), ap(sc4))})
     lin(pc(13), pc(12), 4.0 * K, 0.0)
     lin(pc(14), pc(12), -2000.0, 0.0)
-    lin(pc(15), pc(12), 4.0 * (2 * K + 0.5), 0.0)
-    lin(pc(16), pc(2), 1.0, K + 1.0)
-    lin(W("j4"), W("iot", 0, A, 4), 1.0, pc(16))
-    ts(W("j4"), W("j4"), pc(12), OP.mult, 4.0, OP.mult)
+    lin(pc(15), pc(12), -4000.0 * (2 * K + 0.5), 0.0)
+    lin(pc(16), pc(2), 4.0, 4.0 * (K + 1))
+    lin(W("j4"), W("iot", 0, A, 4), 4.0, pc(16))
+    lin(W("j4"), W("j4"), pc(12), 0.0)
     fill(W("zt"), 0)
     fill(W("ft", 128, 512), 0)
     fill(W("mt", 4 * MC), 0)
@@ -299,10 +307,7 @@ def calls(core, T, topo):
 
     def marks(t):
         quant(W("xq"), W("xs"), X(t))
-        if t < R:
-            mm(0, W("uq"), W("us"), W("xq"), W("xs"))
-        else:
-            mm(0, W("vq"), W("vs"), W("xq"), W("xs"))
+        mm(0, W("uq"), W("us"), W("xq"), W("xs"))
 
     def one_round(t):
         xt, ca, a, hs, ax = "xt%d" % t, "ca%d" % t, SPLIT[t], DC + K * t, AX[t]
@@ -318,7 +323,9 @@ def calls(core, T, topo):
             if t == 2:
                 ts(W("oj"), DS(t, 1), SH + 0.25, OP.add)
                 cp(IND(W("ca2", A), W("oj")), places)
-            ts(nm, W(ca, ax, ax + A), K + 8.0, OP.is_gt)
+            acc, top = (IND(W("at0"), adu[0]), K + 1.0) if t == 0 else (W(ca, ax, ax + A), A + 1.0)
+            node([acc], [nm], {"v": lambda e: e.tensor_scalar(ap(nm), ap(acc), K + 8.0, None, OP.is_gt),
+                               "s": lambda e: e.activation(ap(nm), ap(acc), AF.Relu, scale=1.0 / top, bias=-K / top)})
         scan(W(ca, 0, ax), W(nm[0], nm[1], nm[1] + ax), W("cap", 0, ax), float(K), OP.add, OP.min)
         for i in range(2):
             act(B("sj", t, ax * i, ax * i + ax - 1), W(ca, 0, ax - 1), AF.Sign, -1.0, pc(6 + i), B("js", t, i, i + 1))
@@ -340,7 +347,7 @@ def calls(core, T, topo):
             send(asker, owner, "a_f%d" % t, [(bytes_of("lq", lq, lq + K), bytes_of("fq", 128 * t + q0, 128 * t + q0 + K)),
                                              (W("lsn", ls, ls + 128), W("fs", 128 * t, 128 * t + 128))])
         if t == 0:
-            move(W("jd1", 0, K), IND(INV(1, K), B("alu", 0)))
+            copy("c_jd", W("jd1", 0, K), W("jw1", P, P + K))
             cp(IND(W("at0"), B("alu", 0)), W("prow", 0, K))
             move(W("v1"), IND(W("at0"), adu[1]))
             scan(W("v16"), W("sel16", 0, A), W("v1"), 0.0, OP.mult, OP.add)
@@ -361,11 +368,11 @@ def calls(core, T, topo):
         if t == 0:
             tt(zm[0], cl, al, OP.min)
         elif t == 1:
-            ts(zm[2], al, 1000.0, OP.mult, pc(14), OP.add)
+            lin(zm[2], al, 1000.0, pc(14))
             tt(zm[1], zm[2], cl, OP.min)
             tt(zm[0], zm[1], W("v4m"), OP.max)
         else:
-            ts(zm[2], cl, pc(15), OP.subtract, 1000.0, OP.mult)
+            lin(zm[2], cl, 1000.0, pc(15))
             tt(zm[1], zm[2], W("j4"), OP.max)
             tt(zm[0], zm[1], al, OP.min)
         ts(B("zo", t), zm[0], sc4, OP.mult, pc(10 if t == 1 else 4), OP.add)
@@ -380,7 +387,7 @@ def calls(core, T, topo):
                                 "v": lambda q, out=out, src=src: q.tensor_scalar(ap(out), ap(src), 0.0, 0.03125, OP.max, OP.mult)})
         move(W(xt, 4 * hs, 4 * hs + 4 * K), IND(W(xt, 0, 4 * ax), B("lst", t, 8, 16)))
         if t == 0:
-            move(W("xt1", 4 * (XC - K), 4 * XC), IND(W(xt, 0, 4 * ax), B("lst", t, 8, 16)))
+            copy("c_hs", W("xt1", 4 * (XC - K), 4 * XC), W(xt, 4 * hs, 4 * hs + 4 * K))
         for c in range(16):
             h, piv, o = 16 * c + 16, B("pv", t, 16 * c + 15, 16 * c + 16), P * c
             lo, hi = W("cmp", o, o + h), W("cmp", o + h, o + P)
@@ -395,7 +402,11 @@ def calls(core, T, topo):
                     ts(hi, B("kk", t, h, P), piv, OP.is_lt)
                 scan(W("cnt", 128 * c, 128 * c + 128), W("cmp", o, o + 128), W("cmp", o + 128, o + P), 0.0, OP.add, OP.add)
         tt(B("eqd", t), B("pv", t), B("kk", t), OP.is_equal)
-        scan(B("cor", t), k16[t], B("eqd", t), 0.0, OP.min, OP.add)
+        was = SPLIT[t - 1] if t else 16
+        if a != was:
+            lo, hi = 16 * min(a, was), 16 * max(a, was)
+            lin(W("k16", lo, hi, 16), W("prow", K + lo, K + hi, 16), -1.0 * (a < was), float(-PV - 16) * (a < was))
+        scan(B("cor", t), W("k16"), B("eqd", t), 0.0, OP.min, OP.add)
         ts(B("th", t, 0, 1), W(ca, A - 1, A), 2.0 * K, OP.min, -x0 - K - 0.5, OP.add)
         tt(B("e1", t), B("cor", t, 15, P, 16), B("xx", t), OP.add)
         tt(DS(t, 0, 0, a), W("cnt", 127, 128 * a, 128), B("e1", t, 0, a), OP.subtract)
@@ -408,19 +419,22 @@ def calls(core, T, topo):
         nx = X(t + 1)
         for e in range(4):
             ts(B("xo", t, 16 * e, 16 * e + 16), DS(t + 1, 1), 4.0, OP.mult, 4.0 * SH + e + 0.25, OP.add)
-            move(W(nx[0], nx[1] + e, nx[2], 4), IND(W(xt, 0, 4 * hs + 4 * K), B("xo", t, 16 * e, 16 * e + 16)))
+            for a, b in ([(0, 16)] if t < R - 1 else [(0, 8), (8, 16)]):
+                move(W(nx[0], nx[1] + 64 * a + e, nx[1] + 64 * b, 4), IND(W(xt, 0, 4 * hs + 4 * K), B("xo", t, 16 * e + a, 16 * e + b)))
 
     for t in range(R):
         one_round(t)
 
-    marks(R)
     move(W("otb"), IND(W("tw", 0, P + R * K), B("tpu", R - 1)))
     dma("st", [W("otb")], [], T.ot[:], T.otb[0:128:16, :])
-    dma("st", [W("xq")], [], T.oc[:], ap(RAW(W("xq"), dt.uint8)))
+    for a in (0, 128):
+        quant(W("xq", a, a + 128), W("xs", a, a + 128), W("xt3", 4 * a, 4 * a + 512))
+        mm(a // 128, W("vq"), W("vs"), W("xq", a, a + 128), W("xs", a, a + 128))
+        move(W("yb", a, a + 128), bank(a // 128, 0, 128))
+        dma("st", [W("yb", a, a + 128)], [], T.y[:, a:a + 128], T.yb[:, a:a + 128])
+        dma("st", [W("xq", a, a + 128)], [], T.oc[:, 4 * a:4 * a + 512], ap(bytes_of("xq", a, a + 128)))
     for i in range(4):
         dma("st", [W("xs")], [], T.osc[4 * i:4 * i + 4, :], T.xs[32 * i:32 * i + 4, :])
-    move(W("yb"), pm)
-    dma("st", [W("yb")], [], T.y[:], T.yb[:])
     return nodes
 
 
@@ -446,7 +460,7 @@ def rank_program(g, core, T, topo):
             event[i] = nd["arrival"] + ({},)
             total[event[i][0]] = event[i][1]
             continue
-        need(q, [event[j] for j in nd["deps"]])
+        need(q, [event[j] for j in nd["deps"] if j in event])
         ins = nd["alts"][q](queue[q])
         s = nd["sem"] or "c" + q
         total[s] = total.get(s, 0) + nd["inc"]

from concourse.bass import DstId, RemoteDMATransfer
from concourse.mybir import dt, AluOpType as OP, ActivationFunctionType as AF

MC, P, A, K, R = 768, 256, 192, 32, 3
CODE, U8, U16, BF, F32, I32 = "float8_e4m3fn_x4", "uint8", "uint16", "bfloat16", "float32", "int32"
XC, DC = A, A + P
ZC = [DC + K, DC + K, DC + A]
AX = [A + K, A, A]
AW = [MC + K, MC + 2 * K + A, MC + 2 * K + 2 * A]
PV = P - 1 - K
SH = 1024
UNIT, LIFT = 2.0 ** 70, 2.0 ** 30
SPLIT = [8, 11, 10]
ORDER = """
8g 0s 16v 3y 1y 2s 4y 9g 6y 23v 24v 22v 17v 10g 11s 13s 25v 20v 21g 38v 34s 61v 31s 12g 30s 39s 44s 76v 32v 46v 80v 50s
14s 45g 33s 57s 26s 37s 49s 47s 48s 40s 77v 91v 29s 78g 112s 83v 92s 81s 113v 138v 115s 93v 114s 51v 151v 108s 139p 15g 52v 116v 42v 69g
41v 82s 140v 79x 141v 118s 117s 142v 36s 119v 182v 203s 120v 180v 200s 121g 177v 215s 214v 63g 191s 66g 206s 62g 188v 197s 122x 43v 18g 209s 198s 183v
192s 168v 207s 179v 167v 202s 216v 204s 184v 170v 171v 123v 127s 109v 205s 194s 128v 189v 27s 129g 185v 193s 174v 110s 199s 70g 172v 201s 173v 218v 176v 211s
124v 212s 190v 85v 195s 210s 35s 196s 208s 60g 213s 186v 169v 175v 125s 178v 181v 187v 217v 131s 220v 5s 130x 88s 152v 111v 219v 221v 132v 65g 72v 133s
222v 67g 153v 71v 19g 223v 75v 84s 224v 74v 231v 134v 73v 233s 229v 143p 135v 53v 145p 99v 149p 146s 144s 237v 147p 150s 148s 97v 154s 64g 238v 155v
239s 234v 240s 156v 241v 160p 243s 242v 100s 159p 244v 225v 245v 158p 268v 163s 246g 227v 157p 95v 28s 164s 162v 55s 101v 87v 161s 165s 247x 333s 269s 166y
232s 230v 228s 226v 251s 255v 54s 86s 252v 256p 126v 253g 136v 248v 98s 137v 68g 270v 257v 102s 258v 96s 271v 259v 89s 103v 289v 106g 288v 321s 272v 316v
104g 313v 318s 254x 294v 306v 335v 322s 286v 330s 292v 319s 300v 301v 235s 304v 58s 327s 295v 107x 331s 332v 260p 7s 264p 309v 261s 324s 266p 285v 297v 290v
262p 56v 265s 334v 267s 291v 263s 298v 329s 274s 296v 310v 336v 236v 315v 249v 303v 312v 273s 305v 287v 307v 105x 320s 328s 275v 317v 325s 308v 277p 299v 314v
302v 444s 311v 326s 276p 338v 323s 293v 339v 278p 337v 280s 94v 340v 279p 250v 282s 341v 281v 371p 283s 342v 343v 349v 373p 351s 345v 284v 375p 347v 350v 346s
348v 344s 352v 366v 353s 374s 372v 367p 90s 354v 355v 377p 368v 59s 376s 369v 378s 370v 356v 426s 438s 432s 440s 427s 439s 396v 418v 357v 441s 417v 358v 429s
400v 360s 379v 397v 380s 435s 406v 381v 359s 398v 421v 433s 382v 408v 436s 415v 383v 361v 431s 403v 384s 399v 443v 420v 385s 423v 401v 445v 402v 424v 414v 419v
442s 404v 386v 430s 405v 447v 388p 411v 437s 409v 428s 434s 387p 407v 363s 412v 362s 449v 390p 410v 392s 425v 416v 413v 391s 389p 422v 364v 450v 394s 446v 448v
365v 393s 451v 452v 395s 460v 454v 463v 457v 462v 456s 465v 459s 458v 461s 473v 464s 455v 474p 477y 453v 468v 475s 466s 469p 472y 478y 481y 479y 476y 480y 470v
471s 467y
"""
PER_ROUND = {"jl": (P, F32), "xx": (16, F32), "nm": (A + K, BF), "sj": (2 * (A + K), BF), "js": (2, F32),
             "jo": (2, U16), "gs": (64, F32), "lst": (16, U16), "al": (K, F32), "alu": (2, U16), "zl": (2 * A + K, BF), "zm": (4 * 48, F32), "zo": (48, U16),
             "zz": (4 * A, BF), "m2": (P, F32), "pv": (P, F32), "kk": (P, F32), "eqd": (P, BF), "cor": (P, BF), "ra": (16, F32), "gb": (16, F32),
             "e1": (16, F32), "e2": (16, F32), "th": (2, F32), "tpu": (16, U16), "xo": (64, U16)}
WIDTH = {
    "tg32": (16, I32), "ad32": (36, I32), "tgu": (16, U16), "adu": (36, U16), "lr": (16, U16), "l2r": (16, U16), "l2o": (48, U16),
    "mt": (4 * (MC + K), BF), "ft": (640, BF), "ft2": (4 * A, BF), "fq": (256 + A, CODE), "fs": (256 + A, U8),
    "lq": (192 + A, CODE), "lsn": (384 + A, U8), "zt": (512, BF),
    "ones": (528, BF), "strip": (528, BF), "eq": (512, CODE), "es": (512, U8),
    "ut": (512, BF), "vt": (512, BF), "uq0": (128, CODE), "us0": (128, U8), "uq": (128, CODE), "us": (128, U8),
    "vq": (128, CODE), "vs": (128, U8), "uoff": (8, U16), "wq": (512, CODE), "wsn": (512, U8),
    "xt0": (4 * (ZC[0] + 4), BF), "xt1": (4 * (ZC[1] + K), BF), "xt2": (4 * (ZC[2] + 4), BF), "xt3": (4 * P, BF),
    "xq": (P, CODE), "xs": (P, U8), "zq": (A, CODE), "zs": (A, U8),
    "iot": (AW[2] + A, F32), "inv": (R * (MC + K), F32), "at0": (MC + K, BF), "cap": (A + K, BF), "prow": (K + P, BF), "yrow": (P, F32),
    "ca0": (2 * A + K, BF), "ca1": (2 * A, BF), "ca2": (A + DC, BF), "oj": (16, U16),
    "jd0": (P, F32), "jd1": (P + 2 * K + 8, F32), "jd2": (P, F32), "v1": (A, BF), "v16": (A, BF), "v4": (A, BF), "v4m": (48, F32), "pl": (12, U16), "j4": (48, F32),
    "pat16": (P, BF), "sa": (P, BF), "sb": (P, BF), "sel16": (P, BF), "sel4": (2 * A + K, BF), "c16": (P, BF), "r16": (P, BF), "k16": (P, BF),
    "pi": (4, I32), "pj": (4, I32), "pc": (24, F32), "t4": (16, F32), "pd": (16, F32), "ds": (48 * (R + 1), F32), "d0": (48, F32),
    "jw1": (P + K, F32), "jw2": (P + 2 * K, F32), "tw": (P + 4 * K, F32), "cmp": (16 * P, BF), "cnt": (16 * 128, BF),
    "yb": (P, F32), "otb": (P, F32), "ps": (4096, F32),
}
for _n in PER_ROUND:
    WIDTH[_n] = (R * PER_ROUND[_n][0], PER_ROUND[_n][1])
SCRATCH = {_n: ("psum" if _n == "ps" else "sbuf", [128, WIDTH[_n][0]], WIDTH[_n][1]) for _n in WIDTH}
LOADS = ["tg", "ad", "x", "u", "m", "wc", "ws", "v"]
SEMAPHORES = ["cv", "cs", "cp", "cg", "sent", "st", "a_l0", "a_l1", "a_l2", "a_f0", "a_f1", "a_f2", "a_s2", "c_jd", "c_hs"] + ["ld_" + n for n in LOADS]


def W(name, a=0, b=None, step=1):
    return (name, a, WIDTH[name][0] if b is None else b, step)


def B(name, t, a=0, b=None, step=1):
    w = PER_ROUND[name][0]
    return (name, w * t + a, w * t + (w if b is None else b), step)


def IND(win, off):
    return ("@", win, off)


def RAW(view, d):
    return ("#", view, d)


def calls(core, T, topo):
    rank, n = T.rank_of(core), len(T.cores)
    owner, asker = T.cores[(rank + 1) % n], T.cores[(rank - 1) % n]
    nodes, touched, sends = [], {}, []

    def ap(x):
        if not isinstance(x, tuple):
            return x
        if x[0] == "@":
            return ap(x[1]).indirect(ap(x[2]))
        if x[0] == "#":
            return ap(x[1]).bitcast(x[2])
        return T[x[0]][:, x[1]:x[2]] if x[3] == 1 else T[x[0]][:, x[1]:x[2]:x[3]]

    def plain(xs):
        o = []
        for x in xs:
            if isinstance(x, tuple):
                o += plain(x[1:]) if x[0] in "@#" else [x]
        return o

    def node(rd, wr, alts, tag="", sem=None, inc=1, arrival=None, after=()):
        rd = plain(rd) + plain([x[2] for x in wr if x[0] == "@"])
        wr = plain([x[1] if x[0] == "@" else x for x in wr])
        deps, i = set(after), len(nodes)
        for views, writes in ((rd, False), (wr, True)):
            for name, a, b, s in views:
                m = ((1 << (b - a)) - 1) << a if s == 1 else sum(1 << e for e in range(a, b, s))
                log = touched.setdefault(name, [])
                deps |= set(j for j, m2, w in log if m2 & m and (w or writes) and j != i)
                if writes:
                    log[:] = [(j, m2 & ~m, w) for j, m2, w in log if m2 & ~m]
                log.append((i, m, writes))
        nodes.append({"deps": sorted(deps), "alts": alts, "sem": sem, "inc": inc, "arrival": arrival, "tag": tag or (wr[0][0] if wr else "")})
        return i

    def lanes(src, dst):
        return topo.engines(src, dst)[:8]

    def bits(es):
        return sum(1 << e for e in es)

    def send(dst, src, sem, pairs):
        rid, pid = topo.addr(dst, core)
        es = lanes(core, dst)

        def f(e):
            if len(pairs) == 1:
                return e.remote_dma(ap(pairs[0][0]), ap(pairs[0][1]), T.sem[sem], T.sem.sent, pid, rid, bits(es))
            h = len(es) // 2
            return e.remote_dma_fused([RemoteDMATransfer(dst_ids=[DstId(rid=rid, pnc=pid)], dma_engine_mask=bits(es[h * i:h * i + h]), remote_sem=T.sem[sem],
                                                         src=ap(pairs[i][1]), dst=ap(pairs[i][0])) for i in range(2)], local_sem=T.sem.sent)
        i = node([p[1] for p in pairs], [], {"g": f}, "send " + sem, sem="sent", inc=len(es), after=sends[:1])
        sends.append(i)
        node([], [p[0] for p in pairs], {"x": None}, sem, arrival=(sem, len(lanes(src, core))), after=[i])

    def ts(out, a, s1, o1, s2=None, o2=None):
        if s2 is None:
            node([a, s1], [out], {"v": lambda e: e.tensor_scalar(ap(out), ap(a), ap(s1), None, o1)})
        else:
            node([a, s1, s2], [out], {"v": lambda e: e.tensor_scalar(ap(out), ap(a), ap(s1), ap(s2), o1, o2)})

    def tt(out, a, b, o):
        node([a, b], [out], {"v": lambda e: e.tensor_tensor(ap(out), ap(a), ap(b), o)})

    def cp(out, a):
        node([a], [out], {"v": lambda e: e.tensor_copy(ap(out), ap(a))})

    def scan(out, a, b, init, o0, o1):
        node([a, b], [out], {"v": lambda e: e.tensor_tensor_scan(ap(out), ap(a), ap(b), init, o0, o1)})

    def quant(q, s, a):
        node([a], [q, s], {"v": lambda e: e.quantize_mx(ap(q), ap(s), ap(a))})

    def act(out, a, f, scale=1.0, bias=0.0, total=None):
        if total is None:
            node([a, scale, bias], [out], {"s": lambda e: e.activation(ap(out), ap(a), f, scale=ap(scale), bias=ap(bias))})
        else:
            node([a, scale, bias], [out, total], {"s": lambda e: e.activation(ap(out), ap(a), f, scale=ap(scale), bias=ap(bias), accum_out=ap(total))})

    def move(out, a):
        node([a], [out], {"s": lambda e: e.activation(ap(out), ap(a), AF.Copy), "v": lambda e: e.tensor_copy(ap(out), ap(a))})

    def lin(out, a, scale, bias):
        node([a, scale, bias], [out], {"s": lambda e: e.activation(ap(out), ap(a), AF.Identity, scale=ap(scale), bias=ap(bias)),
                                       "v": lambda e: e.tensor_scalar(ap(out), ap(a), ap(scale), ap(bias), OP.mult, OP.add)})

    def steps(out, pattern, base):
        node([], [out], {"g": lambda e: e.iota(ap(out), pattern, base, 0, allow_small_or_imprecise_dtypes=True)})

    def fill(out, c):
        node([], [out], {"g": lambda e: e.iota(ap(out), [[0, out[2] - out[1]]], c, 0, allow_small_or_imprecise_dtypes=True),
                         "v": lambda e: e.memset(ap(out), float(c))})

    def bank(b, a=0, w=512):
        return W("ps", 512 * b + a, 512 * b + a + w)

    def mm(b, w, ws, x, xs):
        node([w, ws, x, xs], [bank(b)], {"p": lambda e: e.matmul_mx(ap(bank(b, 0, x[2] - x[1])), ap(w), ap(ws), ap(x), ap(xs), True, True)})

    def dma(sem, rd, wr, out, a):
        node(rd, wr, {"y": lambda e: e.dma_start(out, a), "s": lambda e: e.dma_start(out, a)}, sem, sem=sem, inc=16)

    def load(name, view):
        dma("ld_" + name, [], [view], ap(view), T[name][:])

    def copy(sem, out, a):
        dma(sem, [a], [out], ap(out), ap(a))

    def ramp(out, width, base, src):
        node([src], [out], {"g": lambda e: e.iota(ap(out), [[1, width]], base, 0, allow_small_or_imprecise_dtypes=True),
                            "s": lambda e: e.activation(ap(out), ap(src), AF.Identity, bias=float(base + P - 1)),
                            "v": lambda e: e.tensor_scalar(ap(out), ap(src), float(base + P - 1), None, OP.add)})

    def pc(i):
        return W("pc", i, i + 1)

    def X(t):
        return W("xt%d" % t, 4 * XC, 4 * DC) if t < R else W("xt3")

    def DS(t, e=0, a=0, b=16):
        return W("ds", 48 * t + 3 * a + e, 48 * t + 3 * b, 3)

    def INV(t, more=0):
        return W("inv", (MC + K) * t, (MC + K) * t + MC + more)

    def bytes_of(name, a, b):
        return RAW(W(name, a, b), dt.uint8)

    pm = bank(0, 0, P)
    adu = [W("adu", 12 * t, 12 * t + 12) for t in range(R)]
    places = W("prow", K)
    jd = [W("jd0"), W("jd1", K, K + P), W("jd2")]

    load("tg", W("tg32"))
    load("ad", W("ad32"))
    load("x", X(0))
    load("u", W("ut"))
    load("m", W("mt", 0, 4 * MC))
    load("wc", RAW(W("wq"), dt.uint8))
    load("ws", W("wsn"))
    load("v", W("vt"))

    node([], [W("pi", 0, 1)], {"g": lambda e: e.iota(ap(W("pi", 0, 1)), [[0, 1]], 0, 1)})
    steps(W("prow"), [[1, K + P]], 1 - P)
    steps(W("pat16"), [[0, 16], [1, 16]], 0)
    for a in range(0, MC + K, K + P):
        w = min(K + P, MC + K - a)
        ramp(W("iot", a, a + w), w, a, W("prow", 0, w))
    ramp(W("iot", AW[0] + A, AW[1]), K, MC, W("prow", 0, K))
    steps(W("d0"), [[0, 16], [30000, 3]], -30000)
    fill(W("at0"), 2 * K + 1)
    fill(INV(0), 0)
    fill(INV(1, K), 0)
    fill(INV(2, K), 0)
    fill(W("cap"), 2 * K + 1)
    fill(B("nm", 0, A), 1)
    ts(W("pj", 0, 1), W("pi", 0, 1), 15, OP.bitwise_and)
    ts(W("pj", 1, 2), W("pi", 0, 1), 3, OP.bitwise_and)
    ts(W("pj", 2, 3), W("pi", 0, 1), 2, OP.logical_shift_right, 3, OP.bitwise_and)
    cp(W("pc", 0, 3), W("pj", 0, 3))
    lin(pc(3), pc(0), 1.0, 1.0)
    lin(pc(4), pc(1), 1.0, 4.0 * PV + 0.25)
    lin(pc(10), pc(1), 1.0, 4.0 * (PV + K) + 0.25)
    lin(pc(5), pc(1), 1.0, 0.25)
    lin(pc(6), pc(0), 1.0, K + 0.5)
    lin(pc(7), pc(0), 1.0, K + 16.5)
    ts(pc(9), pc(0), 15.0, OP.is_equal, 1.0 / LIFT, OP.max)
    lin(pc(8), pc(9), -1.0 / UNIT, 0.0)
    lin(pc(11), pc(0), 1.0, float(XC - SH + PV))
    lin(W("pd"), W("prow", K, K + P, 16), 1.0, pc(11))
    lin(DS(0, 2), W("prow", K, K + P, 16), 1.0, pc(11))
    lin(W("yrow"), places, -UNIT, (2 * SH - DC - PV) * UNIT)
    ts(W("uoff"), W("prow", K, K + 128, 16), float(PV), OP.add)
    lin(pc(17), pc(0), -2.0 ** 90, 0.0)
    node([W("pat16"), pc(0), pc(17)], [W("c16")], {"v": lambda e: e.tensor_scalar(ap(W("c16")), ap(W("pat16")), ap(pc(0)), 2.0 ** 90, OP.not_equal, OP.mult),
                                                   "s": lambda e: e.activation(ap(W("c16")), ap(W("pat16")), AF.Abs, scale=2.0 ** 90, bias=ap(pc(17)))})
    ts(W("sa"), W("pat16"), pc(0), OP.not_equal)
    ts(W("sb"), W("pat16"), pc(3), OP.is_equal, LIFT, OP.mult)
    tt(W("sel16"), W("sa"), W("sb"), OP.max)
    lin(W("r16"), W("pat16"), -2.0 ** 96, 2.0 ** 95)
    steps(W("k16"), [[0, 16], [512, 16]], 0)
    ts(W("t4", 8, 12), W("pat16", 0, 4), pc(2), OP.is_gt, 2.0 ** 20, OP.mult)
    for e in range(4):
        lin(W("sel4", e, 2 * A + K, 4), W("prow", 0, (2 * A + K) // 4), 0.0, W("t4", 8 + e, 9 + e))
    ts(W("t4", 0, 4), W("pat16", 0, 4), pc(2), OP.is_le, 2.0 ** -10, OP.max)
    scan(W("t4", 4, 8), W("t4", 0, 4), W("t4", 0, 4), 4.0, OP.mult, OP.mult)
    sc4 = W("t4", 7, 8)
    node([sc4], [pc(12)], {"v": lambda e: e.reciprocal(ap(pc(12)), ap(sc4))})
    lin(pc(13), pc(12), 4.0 * K, 0.0)
    lin(pc(14), pc(12), -2000.0, 0.0)
    lin(pc(15), pc(12), -4000.0 * (2 * K + 0.5), 0.0)
    lin(pc(16), pc(2), 4.0, 4.0 * (K + 1))
    lin(W("j4"), W("iot", 0, A, 4), 4.0, pc(16))
    lin(W("j4"), W("j4"), pc(12), 0.0)
    fill(W("zt"), 0)
    fill(W("ft", 128, 512), 0)
    fill(W("mt", 4 * MC), 0)
    for t in range(R):
        fill(W("xt%d" % t, 4 * ZC[t], 4 * ZC[t] + 16), 0)
    fill(W("ra"), 0)
    fill(W("jd1", K + P), 0)
    fill(W("ca2", A, 2 * A), K + 1 + A)
    fill(W("ones"), 1)
    node([W("ones")], [W("strip")], {"g": lambda e: e.affine_select(ap(W("strip")), ap(W("ones")), [[1, 528]], OP.is_equal, 0.0, -3, -4)})
    for b in range(4):
        quant(W("eq", 128 * b, 128 * b + 128), W("es", 128 * b, 128 * b + 128), W("strip", 3 - b, 3 - b + 512))
    quant(W("lq", 32, 160), W("lsn", 128, 256), W("zt"))

    cp(W("tgu"), W("tg32"))
    cp(W("adu"), W("ad32"))
    send(owner, asker, "a_l2", [(W("l2r", 0, 12), adu[2])])
    cp(IND(W("at0"), W("tgu")), places)
    move(W("ca0", AX[0]), IND(W("at0"), adu[0]))
    for t in range(R):
        move(W("iot", AW[t], AW[t] + A), IND(W("iot", 0, MC), adu[t]))
        cp(IND(INV(t), adu[t]), W("yrow", K * t, K * t + A))
    move(W("jw1", 0, P), IND(INV(1), W("tgu")))
    move(W("jw2", 0, P), IND(INV(2), W("tgu")))
    move(W("tw", 0, P), IND(W("iot", 0, MC), W("tgu")))
    quant(W("uq0"), W("us0"), W("ut"))
    move(W("us"), IND(W("us0"), W("uoff")))
    cp(RAW(W("uq"), dt.uint32), IND(RAW(W("uq0"), dt.uint32), W("uoff")))
    quant(W("vq"), W("vs"), W("vt"))
    for e in range(4):
        ts(W("l2o", 12 * e, 12 * e + 12), W("l2r", 0, 12), 4.0, OP.mult, float(e), OP.add)
        move(W("ft2", e, 4 * A, 4), IND(W("mt", 0, 4 * MC), W("l2o", 12 * e, 12 * e + 12)))
    quant(W("fq", 256), W("fs", 256), W("ft2"))
    send(asker, owner, "a_f2", [(bytes_of("lq", 192, 192 + A), bytes_of("fq", 256, 256 + A))])
    send(asker, owner, "a_s2", [(W("lsn", 384), W("fs", 256))])

    def marks(t):
        quant(W("xq"), W("xs"), X(t))
        mm(0, W("uq"), W("us"), W("xq"), W("xs"))

    def one_round(t):
        xt, ca, a, hs, ax = "xt%d" % t, "ca%d" % t, SPLIT[t], DC + K * t, AX[t]
        x0 = float(SH - hs)
        move(jd[t], IND(INV(0), W("tgu")) if t == 0 else IND(W("jw%d" % t), B("tpu", t - 1)))
        scan(B("jl", t), W("sel16"), jd[t], 0.0, OP.mult, OP.add)
        lin(B("xx", t), B("jl", t, 15, P, 16), pc(8), x0)
        tt(DS(t, 1), B("xx", t), W("pd"), OP.min)
        nm = W("ca1", A) if t == 1 else B("nm", t, 0, A)
        if t == 1:
            tt(nm, IND(W("jd1"), W("pl")), W("yrow", K, K + A), OP.not_equal)
        else:
            if t == 2:
                ts(W("oj"), DS(t, 1), SH + 0.25, OP.add)
                cp(IND(W("ca2", A), W("oj")), places)
            acc, top = (IND(W("at0"), adu[0]), K + 1.0) if t == 0 else (W(ca, ax, ax + A), A + 1.0)
            node([acc], [nm], {"v": lambda e: e.tensor_scalar(ap(nm), ap(acc), K + 8.0, None, OP.is_gt),
                               "s": lambda e: e.activation(ap(nm), ap(acc), AF.Relu, scale=1.0 / top, bias=-K / top)})
        scan(W(ca, 0, ax), W(nm[0], nm[1], nm[1] + ax), W("cap", 0, ax), float(K), OP.add, OP.min)
        for i in range(2):
            act(B("sj", t, ax * i, ax * i + ax - 1), W(ca, 0, ax - 1), AF.Sign, -1.0, pc(6 + i), B("js", t, i, i + 1))
        ts(B("jo", t), B("js", t), 0.5, OP.mult, (ax - 1) / 2 + 0.25, OP.add)
        s = P + K * t
        move(W("tw", s, s + K), IND(W("iot", AW[t], AW[t] + ax), B("jo", t)))
        move(W("tw", s + K, s + 2 * K), IND(W("iot", 0, ax), B("jo", t)))
        scan(B("gs", t), W("sel4", 0, 64), W("tw", s, s + 2 * K), 0.0, OP.mult, OP.add)
        ts(B("lst", t), B("gs", t, 3, 64, 4), sc4, OP.mult, pc(5), OP.add)
        if t < 2:
            send(owner, asker, "a_l%d" % t, [(W("lr", 8 * t, 8 * t + 8), B("lst", t, 0, 8))])
            scan(B("al", t), W("sel16", 0, K), W("tw", s, s + K), 0.0, OP.mult, OP.add)
            ts(B("alu", t), B("al", t, 15, K, 16), pc(9), OP.mult, 0.25, OP.add)
            for i in range(t + 1, R):
                move(W("jw%d" % i, s, s + K), IND(INV(i, K), B("alu", t)))
            f0, q0, lq, ls = [(512, 96, 0, 0), (0, 0, 160, 256)][t]
            move(W("ft", f0, f0 + 128), IND(W("mt"), W("lr", 8 * t, 8 * t + 8)))
            quant(W("fq", 128 * t, 128 * t + 128), W("fs", 128 * t, 128 * t + 128), W("ft", f0 - 4 * q0, f0 - 4 * q0 + 512))
            send(asker, owner, "a_f%d" % t, [(bytes_of("lq", lq, lq + K), bytes_of("fq", 128 * t + q0, 128 * t + q0 + K)),
                                             (W("lsn", ls, ls + 128), W("fs", 128 * t, 128 * t + 128))])
        if t == 0:
            copy("c_jd", W("jd1", 0, K), W("jw1", P, P + K))
            cp(IND(W("at0"), B("alu", 0)), W("prow", 0, K))
            move(W("v1"), IND(W("at0"), adu[1]))
            scan(W("v16"), W("sel16", 0, A), W("v1"), 0.0, OP.mult, OP.add)
            ts(W("pl"), W("v16", 15, A, 16), pc(9), OP.mult, P - 1 + 0.25, OP.add)
            scan(W("v4"), W("sel4", 0, A), W("v1"), 0.0, OP.mult, OP.add)
            ts(W("v4m"), W("v4", 3, A, 4), pc(13), OP.min)
        marks(t)
        tt(B("m2", t), pm, W("c16"), OP.add)
        tt(B("kk", t), pm, jd[t], OP.add)
        scan(B("pv", t), W("r16"), B("m2", t), 0.0, OP.max, OP.min)
        vq, vs, cols, o, w = [(0, 96, 128, 0, K), (64, 160, 128, 96, K), (192, 384, A, 0, A)][t]
        for b in range(4):
            mm(4 + b, W("eq", 128 * b, 128 * b + 128), W("es", 128 * b, 128 * b + 128), W("lq", vq, vq + cols), W("lsn", vs, vs + cols))
            move(W(xt, 4 * DC + b, 4 * (DC + w), 4), bank(4 + b, o, w))
        scan(B("zl", t, 0, ax + A), W("sel4", 0, ax + A), W(ca, 0, ax + A), 0.0, OP.mult, OP.add)
        cl, al = B("zl", t, 3, A, 4), B("zl", t, ax + 3, ax + A, 4)
        zm = [B("zm", t, 48 * i, 48 * i + 48) for i in range(3)]
        if t == 0:
            tt(zm[0], cl, al, OP.min)
        elif t == 1:
            lin(zm[2], al, 1000.0, pc(14))
            tt(zm[1], zm[2], cl, OP.min)
            tt(zm[0], zm[1], W("v4m"), OP.max)
        else:
            lin(zm[2], cl, 1000.0, pc(15))
            tt(zm[1], zm[2], W("j4"), OP.max)
            tt(zm[0], zm[1], al, OP.min)
        ts(B("zo", t), zm[0], sc4, OP.mult, pc(10 if t == 1 else 4), OP.add)
        for h in range(2):
            move(B("zz", t, 384 * h, 384 * h + 384), IND(W(xt, 4 * (XC - K if t == 1 else XC), 4 * ZC[t] + 16), B("zo", t, 24 * h, 24 * h + 24)))
        quant(W("zq"), W("zs"), B("zz", t))
        for b in range(4):
            mm(b, W("wq", 128 * b, 128 * b + 128), W("wsn", 128 * b, 128 * b + 128), W("zq"), W("zs"))
        for b in range(4):
            out, src = W(xt, b, 4 * A, 4), bank(b, 0, A)
            node([src], [out], {"s": lambda q, out=out, src=src: q.activation(ap(out), ap(src), AF.Relu, scale=0.03125),
                                "v": lambda q, out=out, src=src: q.tensor_scalar(ap(out), ap(src), 0.0, 0.03125, OP.max, OP.mult)})
        move(W(xt, 4 * hs, 4 * hs + 4 * K), IND(W(xt, 0, 4 * ax), B("lst", t, 8, 16)))
        if t == 0:
            copy("c_hs", W("xt1", 4 * (XC - K), 4 * XC), W(xt, 4 * hs, 4 * hs + 4 * K))
        for c in range(16):
            h, piv, o = 16 * c + 16, B("pv", t, 16 * c + 15, 16 * c + 16), P * c
            lo, hi = W("cmp", o, o + h), W("cmp", o + h, o + P)
            if c >= a:
                act(W("cmp", o, o + P), B("kk", t), AF.Sign, -1.0, piv)
                act(lo, lo, AF.Relu, -1.0, 0.0, B("gb", t, c, c + 1))
                if h < P:
                    act(hi, hi, AF.Relu, 1.0, 0.0, B("ra", t, c, c + 1))
            else:
                ts(lo, B("kk", t, 0, h), piv, OP.is_le)
                if h < P:
                    ts(hi, B("kk", t, h, P), piv, OP.is_lt)
                scan(W("cnt", 128 * c, 128 * c + 128), W("cmp", o, o + 128), W("cmp", o + 128, o + P), 0.0, OP.add, OP.add)
        tt(B("eqd", t), B("pv", t), B("kk", t), OP.is_equal)
        was = SPLIT[t - 1] if t else 16
        if a != was:
            lo, hi = 16 * min(a, was), 16 * max(a, was)
            lin(W("k16", lo, hi, 16), W("prow", K + lo, K + hi, 16), -1.0 * (a < was), float(-PV - 16) * (a < was))
        scan(B("cor", t), W("k16"), B("eqd", t), 0.0, OP.min, OP.add)
        ts(B("th", t, 0, 1), W(ca, A - 1, A), 2.0 * K, OP.min, -x0 - K - 0.5, OP.add)
        tt(B("e1", t), B("cor", t, 15, P, 16), B("xx", t), OP.add)
        tt(DS(t, 0, 0, a), W("cnt", 127, 128 * a, 128), B("e1", t, 0, a), OP.subtract)
        if a < 16:
            tt(B("e2", t, a, 16), B("gb", t, a, 16), B("e1", t, a, 16), OP.add)
            tt(DS(t, 0, a), B("ra", t, a, 16), B("e2", t, a, 16), OP.subtract)
        ts(W("d0", 1, 48, 3), DS(t), B("th", t, 0, 1), OP.subtract, -4096.0, OP.mult)
        scan(W("ds", 48 * t + 48, 48 * t + 96), W("d0"), W("ds", 48 * t, 48 * t + 48), 0.0, OP.min, OP.max)
        ts(B("tpu", t), DS(t + 1, 2), SH - XC + 0.25, OP.add)
        nx = X(t + 1)
        for e in range(4):
            ts(B("xo", t, 16 * e, 16 * e + 16), DS(t + 1, 1), 4.0, OP.mult, 4.0 * SH + e + 0.25, OP.add)
            for a, b in ([(0, 16)] if t < R - 1 else [(0, 8), (8, 16)]):
                move(W(nx[0], nx[1] + 64 * a + e, nx[1] + 64 * b, 4), IND(W(xt, 0, 4 * hs + 4 * K), B("xo", t, 16 * e + a, 16 * e + b)))

    for t in range(R):
        one_round(t)

    move(W("otb"), IND(W("tw", 0, P + R * K), B("tpu", R - 1)))
    dma("st", [W("otb")], [], T.ot[:], T.otb[0:128:16, :])
    for a in (0, 128):
        quant(W("xq", a, a + 128), W("xs", a, a + 128), W("xt3", 4 * a, 4 * a + 512))
        mm(a // 128, W("vq"), W("vs"), W("xq", a, a + 128), W("xs", a, a + 128))
        move(W("yb", a, a + 128), bank(a // 128, 0, 128))
        dma("st", [W("yb", a, a + 128)], [], T.y[:, a:a + 128], T.yb[:, a:a + 128])
        dma("st", [W("xq", a, a + 128)], [], T.oc[:, 4 * a:4 * a + 512], ap(bytes_of("xq", a, a + 128)))
    for i in range(4):
        dma("st", [W("xs")], [], T.osc[4 * i:4 * i + 4, :], T.xs[32 * i:32 * i + 4, :])
    return nodes


def rank_program(g, core, T, topo):
    if T.rank_of(core) is None:
        return
    nodes = calls(core, T, topo)
    plan = [(int(w[:-1]), w[-1]) for w in ORDER.split()] or [(i, list(nd["alts"])[0]) for i, nd in enumerate(nodes)]
    queue = {"v": g.vector, "s": g.scalar, "p": g.tensor, "g": g, "y": g.sync}
    total, event, known = {}, {}, {q: {} for q in queue}

    def need(q, events):
        for s, v, before in events:
            if known[q].get(s, 0) < v and not any(b.get(s, 0) >= v or (s2 == s and v2 > v) for s2, v2, b in events):
                queue[q].wait_ge(T.sem[s], v)
        for s, v, before in events:
            for s2, v2 in list(before.items()) + [(s, v)]:
                known[q][s2] = max(known[q].get(s2, 0), v2)

    for i, q in plan:
        nd = nodes[i]
        if nd["arrival"]:
            event[i] = nd["arrival"] + ({},)
            total[event[i][0]] = event[i][1]
            continue
        need(q, [event[j] for j in nd["deps"] if j in event])
        ins = nd["alts"][q](queue[q])
        s = nd["sem"] or "c" + q
        total[s] = total.get(s, 0) + nd["inc"]
        if s != "sent":
            ins.then_inc(T.sem[s], nd["inc"])
            event[i] = (s, total[s], dict(known[q]))
    for s in sorted(total):
        need("g", [(s, total[s], {})])
